import numpy as np, ml_dtypes
CORES = [23,119,17,113]
N = 4
import mx_ref
BF = ml_dtypes.bfloat16
def gentries(a):
    return np.ascontiguousarray(a.reshape(8, 16, -1).transpose(0, 2, 1)).reshape(8, -1)
def gtable(e):
    e = np.asarray(e); return np.ascontiguousarray(e.reshape(8, -1, 16).transpose(0, 2, 1)).reshape(128, -1).astype(np.int32)
def gcols(t, e):
    v = np.concatenate([t.reshape(8, 16, -1, 4), np.zeros((8, 16, 1, 4), BF)], axis=2)
    return np.ascontiguousarray(np.stack([v[g][:, e[g]] for g in range(8)])).reshape(128, -1)
def tile(rs):
    return np.stack(rs, axis=2).reshape(128, -1).astype(BF)
def pick(q, e):
    c = np.concatenate([q[0].reshape(128, -1, 4), np.zeros((128, 1, 4), np.uint8)], axis=1); s = np.concatenate([q[1], np.ones((16, 1), np.uint8)], axis=1)
    return (np.ascontiguousarray(c[:, e].reshape(128, -1)), np.ascontiguousarray(s[:, e]))
def join(*qs):
    return (np.concatenate([q[0] for q in qs], axis=1), np.concatenate([q[1] for q in qs], axis=1))
def put(q, e, v):
    c, s = q[0].reshape(128, -1, 4).copy(), q[1].copy(); c[:, e] = v[0].reshape(128, -1, 4); s[:, e] = v[1]
    return (c.reshape(128, -1), s)
def pk(c, s):
    return (np.ascontiguousarray(c), mx_ref.live(s))
def emit(q):
    return q[0], q[1]
def packed(v, rng):
    q = [mx_ref.quantize(np.ascontiguousarray(v[r])) for r in range(N)]
    return np.stack([a for a, b in q]), np.stack([mx_ref.plane(b, rng) for a, b in q])
def values_of_codes():
    e, c = np.zeros((128, 128, 4), np.float32), np.zeros((128, 2, 4), np.uint8)
    e[np.arange(128), np.arange(128), 0] = 1
    c[:127, :, 0] = np.arange(256).reshape(2, 128).T[:127]
    return mx_ref.matmul(mx_ref.quantize(e.reshape(128, 512).astype(BF)), (c.reshape(128, 8), np.full((16, 2), 127, np.uint8))).T.reshape(-1).astype(np.float64)
CODE_VALUE, SCALE_VALUE = values_of_codes(), 2.0 ** (np.arange(256) - 127.0)
def decode(q):
    return (CODE_VALUE[q[0]].reshape(16, 8, -1, 4) * SCALE_VALUE[q[1]][:, None, :, None] + 0.0).reshape(128, -1).astype(np.float32)
def f(rng, *shape):
    return mx_ref.flush((rng.standard_normal(shape, dtype=np.float32) * np.exp2(rng.integers(-2, 3, shape[:-1] + (1,)))).astype(BF))
def wide(rng, *shape, cols=0):
    v = rng.standard_normal(shape, dtype=np.float32) * np.exp2(rng.integers(-12, 13, shape)).astype(np.float32)
    if cols: v *= np.repeat(np.exp2(rng.integers(-cols, cols + 1, shape[:-2] + (1, shape[-1] // 4))) * (rng.random(shape[:-2] + (1, shape[-1] // 4)) > 0.0625), 4, axis=-1).astype(np.float32)
    return mx_ref.flush(v.astype(BF))
C, F = 448, 336
MASK = [1, 2, 3]
def numbers_of(rng):
    return {"x": np.array(f(rng, N, 128, 4 * C)), "u": np.array(f(rng, N, 128, 512)), "v": np.array(f(rng, N, 128, 512))}
def stored(k, n):
    return {"dl": np.stack([gtable(k[r]) for r in range(N)]), "nl": np.stack([gtable(n[r]) for r in range(N)])}
def lists(rng):
    e = np.tile(np.arange(C), (N, 8, 1))
    k, e = rng.permuted(e, axis=2), rng.permuted(e, axis=2)
    n = np.empty_like(e)
    np.put_along_axis(n, e, e.reshape(N, 8, -1, 2)[..., ::-1].reshape(N, 8, C), axis=2)
    return k, n
def layers(rng, still=[]):
    w = np.array(f(rng, N, 128, 2048)).reshape(N, 8, 16, 4, 8, 16, 4)
    for i in still:
        w[:, :, i] = 0
        w[:, :, :, :, :, i] = 0
    return w
def weights(rng, w):
    c, s = packed(np.ascontiguousarray(w).reshape(N, 128, 2048), rng)
    return {"wc": c, "ws": s}
def setup_inputs(rng):
    return {**numbers_of(rng), **stored(*lists(rng)), **weights(rng, layers(rng))}
def setup_inputs_ties(rng):
    d = numbers_of(rng)
    k, n = lists(rng)
    o, h = rng.permutation(N), rng.permutation(8)
    i = np.arange(N)
    e = (i ^ (i >> 1) ^ (i >> 2)) % 2
    s = rng.integers(0, 4, (N, 8, C))
    s[o[1]] += 1
    s[:, h[:3]] = 1
    for g in h[:2]:
        for r in np.flatnonzero(e):
            k[r, g] = n[r, g]
            s[r, g] = np.where(np.arange(C) < n[r, g], 2, 0)
    c = np.ones((N, 8), np.float32)
    c[o[0]] = 0
    c[o[1]] = -1
    c[:, h[:3]] = 1
    x = d["x"].reshape(N, 8, 16, C, 4)
    x[:, :, 0] = 0
    x[:, :, 0, :, 0] = s.astype(np.float32).astype(BF)
    a = np.exp2(rng.integers(-3, 4, (1, 8, 1)).astype(np.float32))
    x[:, :, 8:] = 0
    x[:, :, 8, :, 0] = (-1.125 * a).astype(BF)
    x[:, :, 10, :, 0] = (-0.0703125 * a).astype(BF)
    u = d["u"].reshape(N, 128, 128, 4)
    u[:, :, ::16] = 0
    w = layers(rng, [0])
    w[:, :, :, :, :, 8:] = 0
    for g in range(8):
        u[:, 16 * g, 16 * g, 0] = c[:, g].astype(BF)
        w[:, g, 8, 0, g, 8, 0] = -28.0
        for b in range(4): w[:, g, 10, b, g, 9, 0] = -2.0 ** (b - 5)
    return {"x": x.reshape(N, 128, 4 * C), "u": u.reshape(N, 128, 512), "v": d["v"], **stored(k, n), **weights(rng, w)}
def setup_inputs_near(rng):
    d = numbers_of(rng)
    k, n = lists(rng)
    x = d["x"].astype(np.float32).reshape(N, 8, 16, C, 4)
    x[:, :, 0] = 0
    x[:, :, 8:] = 0
    u = d["u"].reshape(N, 128, 128, 4)
    u[:, :, ::16] = 0
    w = layers(rng, [0, 8, 9, 10, 11, 12, 13, 14, 15])
    at = [0, C - 1, int(rng.integers(C)), int(rng.integers(C))]
    for i, g in enumerate(rng.permutation(8)):
        h, c = 16 * g, 1.0 if i < 2 else 2.0 ** -30
        s = rng.integers(0, 16, (N, C))
        digits = ((s[:, :, None] >> np.arange(4)) & 1) * np.exp2(np.arange(4) - 23.0)
        u[:, h, h, 0] = c
        if i < 4:
            x[:, g, 0, :, 0] = i % 2 * 3.0 - 1.5
            x[:, g, 8] = digits
            x[:, g, 11, :, 0] = 2.0 ** -10
            u[:, h + 11, h, 0] = c
        elif i < 6: x[:, g, 8] = digits * rng.choice([-1.0, 1.0], (N, C, 1))
        else:
            x[:, g, 10, :, 0] = rng.choice([-1.0, 1.0], (N, C)) * 2.0 ** -30
            x[:, g, 11, :, 0] = 2.0 ** -29
            w[:, g, 10, 0, g, 9, 0] = 2.0 ** -9
            w[:, g, 12, 0, g, 9, 0] = 1.0
            w[:, g, 10, 0, g, 13, 0] = -2.0 ** -9
            w[:, g, 12, 0, g, 13, 0] = 1.0
            w[:, g, 11, 0, g, 11, 0] = 16.0
            u[:, h + 9, h, 0] = 1.125 * c
            u[:, h + 13, h, 0] = c
        if i < 6: u[:, h + 8, h] = c
        if i % 2: x[:, g, 0, at[i // 2], 0] = 2.0 ** 29 * rng.choice([-1.0, 1.0], N)
    return {"x": x.reshape(N, 128, 4 * C).astype(BF), "u": u.reshape(N, 128, 512), "v": d["v"], **stored(k, n), **weights(rng, w)}
def setup_inputs_odd(rng):
    d = numbers_of(rng)
    x = (1.0 + (2 * rng.integers(0, 64, (N, 16, 8, C, 4)) + 1) * 2.0 ** -7) * np.exp2(-rng.integers(0, 7, (N, 16, 8, C, 4)).astype(np.float64)) * rng.choice([-1.0, 1.0], (N, 16, 8, C, 4))
    x[:, :, 0, :, 0] = 1.96875 * 2.0 ** 8 * rng.choice([-1.0, 1.0], (N, 16, C))
    x[:, ::2, 1, :, 0] = (8 + rng.integers(0, 2, (N, 8, C))) * 2.0 ** -8
    u = d["u"].reshape(N, 128, 128, 4)
    u[:, :, ::16] = 0
    for h in range(0, 128, 16): u[:, h + 1, h, 0] = 1.0
    return {"x": x.astype(np.float32).reshape(N, 128, 4 * C).astype(BF), "u": u.reshape(N, 128, 512), "v": d["v"], **stored(*lists(rng)), **weights(rng, layers(rng, [0, 8]))}
def setup_inputs_ends(rng):
    d = numbers_of(rng)
    k, n = lists(rng)
    j = np.arange(C)
    o = np.zeros(N, np.int64)
    for i, r in enumerate(rng.permutation([r for r in range(N) if not r & MASK[0]])):
        o[r], o[r ^ MASK[0]] = rng.permutation([1, 2] if i % 2 else [0, 3])
    e, h = rng.permutation(N) % 4, rng.permutation(N) % 4
    k[e == 0] = j
    k[e == 1] = j[::-1]
    k[e == 2] = (j + 1) % C
    n[h == 0] = j[::-1]
    n[h == 1] = j ^ 1
    n[h == 2] = (j + C // 2) % C
    s = rng.choice([-1.0, 1.0], (N, 8, 16, C, 4))
    s[o == 0] = -1
    s[o == 1] = rng.choice([-1.0, 1.0], (N, 1, 1, C, 1))[o == 1]
    x = s * (0.955 + 0.02 * rng.random((N, 8, 16, C, 4))) * 2.0 ** 30
    x[o == 3] = 2.0 ** -30
    g = int(rng.integers(8))
    x[:, g, :8] = 2.0 ** -30
    size = np.where(o == 3, 2.0 ** -30, 2.0 ** 30)
    a = np.stack([rng.permutation(8) % 2 * 2.0 - 1.0 for r in range(N)]) * size[:, None]
    u = d["u"].reshape(N, 128, 128, 4)
    u[:, :, ::16] = a.astype(np.float32).astype(BF)[:, None, :, None]
    v = rng.choice([-1.0, 1.0], (N, 128, 512)) * size[:, None, None]
    w = np.zeros((N, 128, 4, 128, 4), np.float32)
    i, l = np.arange(128), np.arange(16 * g, 16 * g + 8)
    for b in range(4):
        w[:, i, b, i, b] = np.where(o == 3, 32.0, -0.125)[:, None]
        w[:, l, b, l, b] = np.where(o == 3, 256.0, 0.0)[:, None]
    return {"x": x.astype(np.float32).reshape(N, 128, 4 * C).astype(BF), "u": u.reshape(N, 128, 512), "v": v.astype(np.float32).astype(BF), **stored(k, n), **weights(rng, w.astype(BF))}
def setup_inputs_spread(rng):
    d = setup_inputs(rng)
    d["x"] = wide(rng, N, 128, 4 * C, cols=6)
    return d
def check_inputs(d):
    b = []
    for k in ("x", "u", "v"):
        a = np.abs(d[k].astype(np.float32))
        if not (np.isfinite(a).all() and ((a == 0) | (a >= 2.0 ** -30) & (a <= 2.0 ** 30)).all()): b.append("a value of " + k)
    none, least, most = [emit(mx_ref.quantize(np.full((128, 16), k, np.float32).astype(BF)))[1][0, 0] for k in (0.0, 2.0 ** -8, 2.0 ** 8)]
    top = emit(mx_ref.quantize(np.ascontiguousarray(np.tile(np.repeat(1.0 + np.arange(128) * 2.0 ** -7, 4), (128, 1))).astype(np.float32).astype(BF)))[0] & 0x7F
    for r in range(N):
        k, n = gentries(d["dl"][r]), gentries(d["nl"][r])
        if not (np.sort(k, axis=1) == np.arange(C)).all(): b.append("dl: not every column once")
        if not ((n >= 0) & (n < C)).all(): b.append("an entry of nl")
        elif not ((at(n, n) == np.arange(C)) & (n != np.arange(C))).all(): b.append("nl: not in pairs")
        if ((d["wc"][r] == 0x7F) | (d["wc"][r] == 0xFF)).any(): b.append("wc: a code that is no number")
        s = mx_ref.live(d["ws"][r])
        if ((s != none) & ((s < least) | (s > most))).any(): b.append("ws: a scale out of range")
        a = np.max(d["wc"][r].reshape(16, 8, 512, 4) & 0x7F, axis=(1, 3))
        if ((s == none) & (a != 0)).any(): b.append("wc: a code other than zero under the scale of zeros")
        if ((s != none) & ((a < top.min()) | (a > top.max()))).any(): b.append("wc: a block whose largest code isn't one of quantize_mx")
    return b
def at(t, e):
    return np.take_along_axis(t, e, axis=1)
def layer(w, q):
    return tile([mx_ref.matmul(pick(w, np.arange(128 * b, 128 * b + 128)), q) * np.float32(0.03125) for b in range(4)])
def reference(x, u, v, dl, nl, wc, ws):
    qu = [mx_ref.quantize(u[r]) for r in range(N)]
    lay = [pk(wc[r], ws[r]) for r in range(N)]
    d, n = [gentries(dl[r]) for r in range(N)], [gentries(nl[r]) for r in range(N)]
    now = [x[r] for r in range(N)]
    for m in MASK:
        s = [mx_ref.matmul(qu[r], mx_ref.quantize(now[r]))[::16] + np.float32(0.0) for r in range(N)]
        new, h, made = [], [], []
        for r in range(N):
            p = r ^ m
            a, b, k = np.tile(np.arange(C), (8, 1)), n[r], np.zeros((8, C), np.int64)
            for step in range(6):
                own = at(s[r], a) > at(s[p], b)
                a, b, k = np.where(own, at(d[r], a), a), np.where(own, b, at(d[p], b)), k + own
            z = ((gcols(now[r], a).astype(np.float32) + gcols(now[r], b).astype(np.float32)) * np.float32(0.5)).astype(BF)
            h.append(layer(lay[r], mx_ref.quantize(z)))
            new.append(np.where((k + at(k, n[r])) % 2 == 1, at(d[r], n[r]), d[r]))
        for r in range(N):
            p = r ^ m
            far = decode(mx_ref.quantize(np.ascontiguousarray(h[p][:, :4 * F]))).astype(BF)
            both = np.concatenate([far, h[r][:, 4 * F:]], axis=1)
            place = at(np.argsort(d[p], axis=1), new[r])
            made.append((now[r].astype(np.float32) + gcols(both, place).astype(np.float32)).astype(BF))
        now, d = made, new
    y, dn = np.zeros((N, 128, C), np.float32), np.zeros((N, 8, C), np.float32)
    oc, osc = np.zeros((N, 128, 4 * C), np.uint8), np.zeros((N, 16, C), np.uint8)
    for r in range(N):
        q = mx_ref.quantize(now[r])
        y[r] = mx_ref.matmul(mx_ref.quantize(v[r]), q)
        dn[r] = d[r]
        oc[r], osc[r] = emit(q)
    return {"y": y, "dn": dn, "oc": oc, "osc": osc}

@@ -1,0 +1,347 @@
+from concourse.bass import DstId, RemoteDMATransfer
+from concourse.mybir import dt, AluOpType, ActivationFunctionType
+
+C, F, ROUNDS = 448, 336, 3
+K = C // 16
+MASKS = [1, 2, 3]
+CH = [(0, 192), (192, 448)]
+NB = 1 << 9
+NK = 1 << 19
+SLOTS = ["iotaT", "mask", "inv", "dT", "nT", "C0", "h", "P", "hp", "pk", "V1", "U", "V1b", "Ub", "df", "dfo", "eo",
+         "glo", "par", "wd", "wn"] + ["A%d" % i for i in range(1, 6)] + ["B%d" % i for i in range(1, 6)]
+ISLOTS = ["W", "i1", "i2", "is", "odd", "ip", "ib", "dli", "nli"]
+
+SCRATCH = {
+    "sm": ("sbuf", [128, K * len(SLOTS)], "float32"),
+    "si": ("sbuf", [128, K * len(ISLOTS)], "int32"),
+    "xp": ("sbuf", [128, 4 * C], "bfloat16"), "tmp": ("sbuf", [128, 4 * C], "bfloat16"),
+    "z": ("sbuf", [128, 4 * C], "bfloat16"), "hh": ("sbuf", [128, 4 * C], "bfloat16"),
+    "jp": ("sbuf", [128, 4 * C], "bfloat16"),
+    "ub": ("sbuf", [128, 512], "bfloat16"), "vb": ("sbuf", [128, 512], "bfloat16"),
+    "one": ("sbuf", [128, 512], "bfloat16"),
+    "qu": ("sbuf", [128, 128], "float8_e4m3fn_x4"), "su": ("sbuf", [128, 128], "uint8"),
+    "qv": ("sbuf", [128, 128], "float8_e4m3fn_x4"), "sv_": ("sbuf", [128, 128], "uint8"),
+    "qx": ("sbuf", [128, C], "float8_e4m3fn_x4"), "sx": ("sbuf", [128, C], "uint8"),
+    "qz": ("sbuf", [128, C], "float8_e4m3fn_x4"), "sz": ("sbuf", [128, C], "uint8"),
+    "qw": ("sbuf", [128, 512], "float8_e4m3fn_x4"), "sw": ("sbuf", [128, 512], "uint8"),
+    "qe": ("sbuf", [128, 512], "float8_e4m3fn_x4"), "se_": ("sbuf", [128, 512], "uint8"),
+    "ysb": ("sbuf", [128, C], "float32"),
+    "iotaS": ("sbuf", [128, C], "float32"), "nS": ("sbuf", [128, C], "float32"), "neS": ("sbuf", [128, C], "float32"),
+    "einv": ("sbuf", [128, C], "float32"), "m16": ("sbuf", [128, C], "float32"), "rst": ("sbuf", [128, C], "float32"),
+    "c16": ("sbuf", [128, C], "float32"), "gm": ("sbuf", [128, C], "float32"), "sc": ("sbuf", [128, C], "float32"),
+    "ts": ("sbuf", [128, C], "float32"), "tbb": ("sbuf", [128, C], "float32"), "tcb": ("sbuf", [128, C], "float32"),
+    "tfb": ("sbuf", [128, C], "float32"), "sg": ("sbuf", [128, C], "float32"), "te": ("sbuf", [128, C], "float32"),
+    "s480": ("sbuf", [128, C + 32], "float32"), "t480": ("sbuf", [128, C + 32], "float32"),
+    "r480": ("sbuf", [128, C + 32], "float32"), "f480": ("sbuf", [128, C + 32], "float32"),
+    "ph": ("psum", [128, 2048], "float32"), "pd": ("psum", [128, 2048], "float32"),
+    "pq": ("sbuf", [128, 1], "float32"), "pi": ("sbuf", [128, 1], "int32"),
+}
+for _n in ("dW", "nW", "eW", "pW", "aW", "bW", "lW"): SCRATCH[_n] = ("sbuf", [128, K], "uint16")
+for _i in range(4):
+    SCRATCH["x%d" % _i] = ("sbuf", [128, 4 * C], "bfloat16")
+    SCRATCH["et%d" % _i] = ("sbuf", [128, 512], "bfloat16")
+for _i in range(6):
+    SCRATCH["ta%d" % _i] = ("sbuf", [128, C], "float32")
+    SCRATCH["tb%d" % _i] = ("sbuf", [128, C], "float32")
+    SCRATCH["sa%d" % _i] = ("sbuf", [128, C], "float32")
+for _i in range(7): SCRATCH["sb%d" % _i] = ("sbuf", [128, C], "float32")
+for _r in range(ROUNDS):
+    SCRATCH["tsend%d" % _r] = ("sbuf", [128, K], "float32")
+    SCRATCH["tland%d" % _r] = ("sbuf", [128, K], "float32")
+    SCRATCH["lsend%d" % _r] = ("sbuf", [128, 2 * K], "float32")
+    SCRATCH["lland%d" % _r] = ("sbuf", [128, 2 * K], "float32")
+    SCRATCH["qh%d" % _r] = ("sbuf", [128, F], "float8_e4m3fn_x4")
+    SCRATCH["sh%d" % _r] = ("sbuf", [128, F], "uint8")
+    SCRATCH["ql%d" % _r] = ("sbuf", [128, F], "float8_e4m3fn_x4")
+    SCRATCH["sl%d" % _r] = ("sbuf", [128, F], "uint8")
+
+SEMAPHORES = ["qv", "qs", "qt", "qg"] + ["ld%d" % i for i in range(9)] + ["st%d" % i for i in range(7)]
+for _r in range(ROUNDS):
+    for _n in ("t", "l", "c0", "s0", "c1", "s1"): SEMAPHORES += ["a%s%d" % (_n, _r), "o%s%d" % (_n, _r)]
+
+
+def rank_program(g, core, T, topo):
+    rank = T.rank_of(core)
+    if rank is None:
+        return
+    A = AluOpType
+    CP = ActivationFunctionType.Copy
+    eng = {"v": g.vector, "s": g.scalar, "t": g.tensor, "g": g, "y": g.sync}
+    own = {"v": "qv", "s": "qs", "t": "qt", "g": "qg"}
+    count, known, lastw, readers, snap = {}, {q: {} for q in eng}, {}, {}, {}
+
+    def wait(q, ev):
+        s, n = ev
+        if known[q].get(s, 0) >= n: return
+        eng[q].wait_ge(T.sem[s], n)
+        known[q][s] = n
+        for a, b in snap.get(ev, {}).items():
+            if known[q].get(a, 0) < b: known[q][a] = b
+
+    def need(q, r, w):
+        deps = []
+        for k in r: deps += lastw.get(k, [])
+        for k in w:
+            deps += lastw.get(k, [])
+            deps += readers.get(k, [])
+        best = {}
+        for s, n in deps: best[s] = max(n, best.get(s, 0))
+        for s in sorted(best): wait(q, (s, best[s]))
+
+    def done(q, ev, r, w):
+        if q: snap[ev] = dict(known[q])
+        for k in r: readers.setdefault(k, []).append(ev)
+        for k in w: lastw[k], readers[k] = [ev], []
+
+    def op(q, call, r, w):
+        w = w + [k for k in r if k[0] == "P"]
+        r = [k for k in r if k[0] != "P"]
+        need(q, r, w)
+        s = own[q]
+        count[s] = count.get(s, 0) + 1
+        call().then_inc(T.sem[s], 1)
+        done(q, (s, count[s]), r, w)
+
+    def dma(q, sem, out, in_, r, w):
+        need(q, r, w)
+        eng[q].dma_start(out, in_).then_inc(T.sem[sem], 16)
+        count[sem] = 16
+        done(q, (sem, 16), r, w)
+
+    def send(dst, name, out, in_, r):
+        need("g", r, [])
+        m = topo.mask(core, dst)
+        rid, pid = topo.addr(dst)[:2]
+        g.remote_dma(out, in_, T.sem["a" + name], T.sem["o" + name], pid, rid, m)
+        count["o" + name] = len(topo.engines(core, dst))
+        done("g", ("o" + name, count["o" + name]), r, [])
+
+    def arrives(src, name, w):
+        count["a" + name] = len(topo.engines(src, core))
+        for k in w: lastw[k] = [("a" + name, count["a" + name])]
+
+    def sm(n):
+        i = SLOTS.index(n)
+        return T.sm[:, K * i:K * i + K]
+
+    def si(n):
+        i = ISLOTS.index(n)
+        return T.si[:, K * i:K * i + K]
+
+    def col(b, q):
+        return T[b][:, q:C:16]
+
+    def shifted(b, q):
+        return T[b][:, 16 + q:C + q + 1:16]
+
+    def tt(out, a, b, o, r, w): op("v", lambda: g.vector.tensor_tensor(out, a, b, o), r, w)
+    def ts1(out, a, s, o, r, w): op("v", lambda: g.vector.tensor_scalar(out, a, s, None, o), r, w)
+    def ts2(out, a, s, o, s2, o2, r, w): op("v", lambda: g.vector.tensor_scalar(out, a, s, s2, o, o2), r, w)
+    def cp(out, a, r, w): op("v", lambda: g.vector.tensor_copy(out, a), r, w)
+    def tr(out, a, r, w): op("v", lambda: g.vector.transpose(out, a), r, w)
+    def act(out, a, r, w, scale=1.0):
+        if scale == 1.0: op("s", lambda: g.scalar.activation(out, a, CP), r, w)
+        else: op("s", lambda: g.scalar.activation(out, a, CP, scale=scale), r, w)
+    def quant(q, s, t, r, w): op("v", lambda: g.vector.quantize_mx(q, s, t), r, w)
+    def mm(out, a, sa, b, sb, r, w): op("t", lambda: g.tensor.matmul_mx(out, a, sa, b, sb, True, True), r, w)
+    def fill(ap, v, w): op("v", lambda: g.vector.memset(ap, v), [], w)
+    def iota(out, pat, base, cm, w, f=True):
+        if f: op("g", lambda: g.iota(out, pat, base, cm, allow_small_or_imprecise_dtypes=True), [], w)
+        else: op("g", lambda: g.iota(out, pat, base, cm), [], w)
+
+    peer = [T.cores[rank ^ m] for m in MASKS]
+    for r in range(ROUNDS):
+        arrives(peer[r], "t%d" % r, ["tland%d" % r])
+        arrives(peer[r], "l%d" % r, ["lland%d" % r])
+        for k in range(2):
+            arrives(peer[r], "c%d%d" % (k, r), ["ql%d.%d" % (r, k)])
+            arrives(peer[r], "s%d%d" % (k, r), ["sl%d.%d" % (r, k)])
+
+    dma("s", "ld0", si("dli"), T.dl[:, :], [], ["dli"])
+    dma("y", "ld2", T.x0[:, 0:2 * C], T.x[:, 0:2 * C], [], ["x0"])
+    dma("s", "ld1", si("nli"), T.nl[:, :], [], ["nli"])
+    dma("y", "ld3", T.x0[:, 2 * C:4 * C], T.x[:, 2 * C:4 * C], [], ["x0b"])
+    dma("y", "ld4", T.ub[:, :], T.u[:, :], [], ["ub"])
+    dma("y", "ld5", T.qw[:, :].bitcast(dt.uint8), T.wc[:, :], [], ["qw"])
+    dma("y", "ld6", T.sw[:, :], T.ws[:, :], [], ["sw"])
+    dma("y", "ld7", T.vb[:, :], T.v[:, :], [], ["vb"])
+    lastw["x0"] = [("ld2", 16), ("ld3", 16)]
+
+    iota(si("ip"), [[0, K]], 0, 1, ["ip"], False)
+    iota(sm("glo"), [[0, K // 2], [1, 2]], 0, 0, ["glo"])
+    iota(si("ib"), [[32, K // 2], [0, 2]], 0, 0, ["ib"], False)
+    iota(T.iotaS[:, :], [[1, C]], 0, 0, ["iotaS"])
+    iota(T.c16[:, :], [[0, K], [1, 16]], 0, 0, ["c16"])
+    for b in ("ta0", "tbb", "tcb", "tfb"): fill(T[b][:, :], 0.0, [b])
+    for b in ("s480", "r480"): fill(T[b][:, :], 0.0, [b])
+    fill(T.one[:, :], 1.0, ["one"])
+    for b in range(4):
+        op("g", lambda: g.affine_select(T["et%d" % b][:, :], T.one[:, :], [[-1, 512]], A.is_equal, 0.0, b, 4), ["one"], ["et%d" % b])
+    ts2(si("i1"), si("ip"), 4, A.arith_shift_right, 1, A.bitwise_and, ["ip"], ["i1"])
+    cp(sm("par"), si("i1"), ["i1"], ["par"])
+    tt(sm("mask"), sm("par"), sm("glo"), A.is_equal, ["par", "glo"], ["mask"])
+    tt(sm("inv"), sm("par"), sm("glo"), A.not_equal, ["par", "glo"], ["inv"])
+    ts1(si("i2"), si("ip"), 31, A.bitwise_and, ["ip"], ["i2"])
+    tt(sm("iotaT"), si("i2"), si("ib"), A.add, ["i2", "ib"], ["iotaT"])
+
+    def swap(t, s, u, vals, outs):
+        for q, (v, k) in enumerate(vals): cp(col(t, q), v, k, [t])
+        tr(T[s][:, 16:16 + C], T[t][:, :], [t], [s])
+        tr(T[u][:, :], T[s][:, :], [s], [u])
+        for q, ((v, k), (o, ok)) in enumerate(zip(vals, outs)):
+            tt(sm("V1b"), v, sm("mask"), A.mult, k + ["mask"], ["V1b"])
+            tt(sm("Ub"), shifted(u, q), sm("inv"), A.mult, [u, "inv"], ["Ub"])
+            tt(o, sm("V1b"), sm("Ub"), A.add, ["V1b", "Ub"], ok)
+
+    cp(T.dW[:, :], si("dli"), ["dli"], ["dW"])
+    cp(T.lsend0[:, K:2 * K], si("dli"), ["dli"], ["ls0w"])
+    cp(T.nW[:, :], si("nli"), ["nli"], ["nW"])
+    cp(sm("wn"), si("nli"), ["nli"], ["wn"])
+    swap("tfb", "r480", "f480", [(T.lsend0[:, K:2 * K], ["ls0w"]), (sm("wn"), ["wn"])], [(sm("dT"), ["dT"]), (sm("nT"), ["nT"])])
+    cp(T.lsend0[:, 0:K], sm("dT"), ["dT"], ["ls0t"])
+    send(peer[0], "l0", T.lland0[:, :], T.lsend0[:, :], ["ls0w", "ls0t"])
+    ts2(sm("h"), sm("nT"), float(NB), A.mult, 0.0, A.add, ["nT"], ["h"])
+    tt(sm("C0"), sm("h"), sm("iotaT"), A.add, ["h", "iotaT"], ["C0"])
+    tt(col("ta0", 1), sm("iotaT"), sm("dT"), A.subtract, ["iotaT", "dT"], ["ta0"])
+    cp(col("tcb", 1), sm("dT"), ["dT"], ["tcb"])
+    ts1(si("i1"), si("ip"), 15, A.bitwise_and, ["ip"], ["i1"])
+    cp(T.pq[:, :], T.si[:, K * ISLOTS.index("i1"):K * ISLOTS.index("i1") + 1], ["i1"], ["pq"])
+    ts1(T.m16[:, :], T.c16[:, :], T.pq[:, :], A.is_equal, ["c16", "pq"], ["m16"])
+    ts1(T.rst[:, :], T.c16[:, :], 0.0, A.not_equal, ["c16"], ["rst"])
+    act(T.nS[:, :], T.iotaS[:, :].indirect(T.nW[:, :]), ["iotaS", "nW"], ["nS"])
+    quant(T.qu[:, :], T.su[:, :], T.ub[:, :], ["ub"], ["qu"])
+
+    def to_table(win, off, wkeys, out, okey):
+        tt(T.gm[:, :], win.indirect(off), T.m16[:, :], A.mult, wkeys + ["m16"], ["gm"])
+        op("v", lambda: g.vector.tensor_tensor_scan(T.sc[:, :], T.rst[:, :], T.gm[:, :], 0.0, A.mult, A.add), ["rst", "gm"], ["sc"])
+        cp(out, T.sc[:, 15:C:16], ["sc"], [okey])
+
+    for r in range(ROUNDS):
+        p = peer[r]
+        X, XN = "x%d" % r, "x%d" % (r + 1)
+        quant(T.qx[:, :], T.sx[:, :], T[X][:, :], [X], ["qx"])
+        mm(T.pd[:, 0:C], T.qu[:, :], T.su[:, :], T.qx[:, :], T.sx[:, :], ["qu", "qx"], ["Pd0"])
+        for t in range(4): act(T.xp[:, C * t:C * t + C], T[X][:, t:4 * C:4], [X], ["xp%d" % t], 0.5)
+        if r == 0:
+            for b in range(4): quant(T.qe[:, 128 * b:128 * b + 128], T.se_[:, 128 * b:128 * b + 128], T["et%d" % b][:, :], ["et%d" % b], ["qe%d" % b])
+        tr(T.ts[:, :], T.pd[:, 0:C], ["Pd0"], ["ts"])
+        cp(T["tsend%d" % r][:, :], col("ts", 0), ["ts"], ["tsend%d" % r])
+        send(p, "t%d" % r, T["tland%d" % r][:, :], T["tsend%d" % r][:, :], ["tsend%d" % r])
+        cp(col("ta0", 0), col("ts", 0), ["ts"], ["ta0"])
+        tr(T.sa0[:, :], T.ta0[:, :], ["ta0"], ["sa0"])
+        ll = T["lland%d" % r]
+        lk = "lland%d" % r
+
+        def chain_a(i):
+            act(T["sa%d" % i][:, :], T["sa%d" % (i - 1)][:, :].indirect(T.dW[:, :]), ["sa%d" % (i - 1), "dW"], ["sa%d" % i])
+        chain_a(1)
+        chain_a(2)
+        tt(sm("pk"), sm("C0"), col("ta0", 1), A.subtract, ["C0", "ta0"], ["pk"])
+
+        def own_step(i):
+            tr(T["ta%d" % i][:, :], T["sa%d" % i][:, :], ["sa%d" % i], ["ta%d" % i])
+            prev, pkey = (col("ta0", 0), "ta0") if i == 1 else (sm("A%d" % (i - 1)), "A%d" % (i - 1))
+            tt(sm("A%d" % i), prev, col("ta%d" % i, 0), A.min, [pkey, "ta%d" % i], ["A%d" % i])
+            tt(sm("pk"), sm("pk"), col("ta%d" % i, 1), A.subtract, ["pk", "ta%d" % i], ["pk"])
+        own_step(1)
+        cp(T.eW[:, :], ll[:, K:2 * K], [lk], ["eW"])
+        act(T.neS[:, :], T.nS[:, :].indirect(T.eW[:, :]), ["nS", "eW"], ["neS"])
+        for i in (3, 4, 5): chain_a(i)
+        own_step(2)
+        to_table(T.neS[:, :], T.nW[:, :], ["neS", "nW"], T.pW[:, :], "pW")
+        tt(sm("eo"), ll[:, 0:K], sm("iotaT"), A.subtract, [lk, "iotaT"], ["eo"])
+        ts2(col("tbb", 1), sm("eo"), float(NB), A.mult, float(NK), A.add, ["eo"], ["tbb"])
+        own_step(3)
+        own_step(4)
+        cp(col("tbb", 0), T["tland%d" % r][:, :], ["tland%d" % r], ["tbb"])
+        tr(T.sb0[:, :], T.tbb[:, :], ["tbb"], ["sb0"])
+        act(T.sb1[:, :], T.sb0[:, :].indirect(T.nW[:, :]), ["sb0", "nW"], ["sb1"])
+        for j in range(2, 7): act(T["sb%d" % j][:, :], T["sb%d" % (j - 1)][:, :].indirect(T.pW[:, :]), ["sb%d" % (j - 1), "pW"], ["sb%d" % j])
+        own_step(5)
+        for j in range(6):
+            tb, ta = "tb%d" % j, "ta%d" % (5 - j)
+            tr(T[tb][:, :], T["sb%d" % (j + 1)][:, :], ["sb%d" % (j + 1)], [tb])
+            tt(sm("P"), col(tb, 1), col(ta, 1), A.add, [tb, ta], ["P"])
+            if j == 0: bm, bk = col(tb, 0), tb
+            else:
+                pm, pmk = (col("tb0", 0), "tb0") if j == 1 else (sm("B%d" % (j - 1)), "B%d" % (j - 1))
+                bm, bk = sm("B%d" % j), "B%d" % j
+                tt(bm, pm, col(tb, 0), A.min, [pmk, tb], [bk])
+            am, ak = (col("ta0", 0), "ta0") if j == 5 else (sm("A%d" % (5 - j)), "A%d" % (5 - j))
+            tt(sm("h"), am, bm, A.is_le, [ak, bk], ["h"])
+            tt(sm("hp"), sm("h"), sm("P"), A.mult, ["h", "P"], ["hp"])
+            if j < 5: tt(sm("pk"), sm("pk"), sm("hp"), A.add, ["pk", "hp"], ["pk"])
+            else: tt(col("tcb", 0), sm("pk"), sm("hp"), A.add, ["pk", "hp"], ["tcb"])
+        tr(T.s480[:, 16:16 + C], T.tcb[:, :], ["tcb"], ["s480"])
+        tt(sm("V1"), col("tcb", 0), sm("mask"), A.mult, ["tcb", "mask"], ["V1"])
+        tr(T.t480[:, :], T.s480[:, :], ["s480"], ["t480"])
+        tt(sm("U"), shifted("t480", 0), sm("inv"), A.mult, ["t480", "inv"], ["U"])
+        tt(si("W"), sm("V1"), sm("U"), A.add, ["V1", "U"], ["W"])
+        ts1(si("i1"), si("W"), NB - 1, A.bitwise_and, ["W"], ["i1"])
+        cp(T.aW[:, :], si("i1"), ["i1"], ["aW"])
+        ts2(si("i2"), si("W"), 9, A.arith_shift_right, NB - 1, A.bitwise_and, ["W"], ["i2"])
+        cp(T.bW[:, :], si("i2"), ["i2"], ["bW"])
+        for k, (lo, hi) in enumerate(CH):
+            n = hi - lo
+            for t in range(4):
+                win = T.xp[:, C * t:C * t + C]
+                tmp, tk = T.tmp[:, C * t + lo:C * t + hi], "tmp%d%d" % (k, t)
+                act(tmp, win.indirect(T.aW[:, lo // 16:hi // 16]), ["xp%d" % t, "aW"], [tk])
+                tt(T.z[:, 4 * lo + t:4 * hi:4], win.indirect(T.bW[:, lo // 16:hi // 16]), tmp, A.add, ["xp%d" % t, "bW", tk], ["z%d" % k])
+            quant(T.qz[:, lo:hi], T.sz[:, lo:hi], T.z[:, 4 * lo:4 * hi], ["z%d" % k], ["qz%d" % k])
+            for i in range(4):
+                mm(T[("ph", "pd")[k]][:, 512 * i:512 * i + n], T.qw[:, 128 * i:128 * i + 128], T.sw[:, 128 * i:128 * i + 128], T.qz[:, lo:hi], T.sz[:, lo:hi],
+                   ["qw", "sw", "qz%d" % k], ["P" + "hd"[k] + str(i)])
+        for k, (lo, hi) in enumerate(CH):
+            n, far = hi - lo, min(hi, F)
+            for i in range(4):
+                src, dst, pk_ = T[("ph", "pd")[k]][:, 512 * i:512 * i + n], T.hh[:, 4 * lo + i:4 * hi:4], "P" + "hd"[k] + str(i)
+                if k == 0 or i % 2: act(dst, src, [pk_], ["hh%d%d" % (k, i)], 0.03125)
+                else: ts1(dst, src, 0.03125, A.mult, [pk_], ["hh%d%d" % (k, i)])
+            quant(T["qh%d" % r][:, lo:far], T["sh%d" % r][:, lo:far], T.hh[:, 4 * lo:4 * far], ["hh%d%d" % (k, i) for i in range(4)], ["qh%d%d" % (r, k)])
+            send(p, "c%d%d" % (k, r), T["ql%d" % r][:, lo:far].bitcast(dt.uint8), T["qh%d" % r][:, lo:far].bitcast(dt.uint8), ["qh%d%d" % (r, k)])
+            send(p, "s%d%d" % (k, r), T["sl%d" % r][:, lo:far], T["sh%d" % r][:, lo:far], ["qh%d%d" % (r, k)])
+        act(T.sg[:, :], T.s480[:, 16:16 + C].indirect(T.nW[:, :]), ["s480", "nW"], ["sg"])
+        for t in range(4): act(T.jp[:, C * t + F:C * t + C], T.hh[:, 4 * F + t:4 * C:4], ["hh1%d" % t], ["jp%dh" % t])
+        tr(T.te[:, :], T.sg[:, :], ["sg"], ["te"])
+        tt(si("is"), col("tcb", 0), col("te", 0), A.add, ["tcb", "te"], ["is"])
+        ts2(si("odd"), si("is"), 19, A.arith_shift_right, 1, A.bitwise_and, ["is"], ["odd"])
+        tt(sm("df"), col("te", 1), sm("dT"), A.subtract, ["te", "dT"], ["df"])
+        tt(sm("dfo"), sm("df"), si("odd"), A.mult, ["df", "odd"], ["dfo"])
+        tt(sm("dT"), sm("dT"), sm("dfo"), A.add, ["dT", "dfo"], ["dT"])
+        last = r == ROUNDS - 1
+        fw, fk = (sm("wd"), "wd") if last else (T["lsend%d" % (r + 1)][:, K:2 * K], "ls%dw" % (r + 1))
+        swap("tfb", "r480", "f480", [(sm("dT"), ["dT"])], [(fw, [fk])])
+        cp(T.dW[:, :], fw, [fk], ["dW"])
+        if last:
+            dma("y", "st0", T.dn[:, :], T.r480[0:128:16, 16:16 + C], ["r480"], [])
+        else:
+            cp(T["lsend%d" % (r + 1)][:, 0:K], sm("dT"), ["dT"], ["ls%dt" % (r + 1)])
+            send(peer[r + 1], "l%d" % (r + 1), T["lland%d" % (r + 1)][:, :], T["lsend%d" % (r + 1)][:, :], ["ls%dw" % (r + 1), "ls%dt" % (r + 1)])
+        op("v", lambda: g.vector.tensor_copy(T.einv[:, :].indirect(T.eW[:, :]), T.iotaS[:, :]), ["eW", "iotaS"], ["einv"])
+        to_table(T.einv[:, :], T.dW[:, :], ["einv", "dW"], T.lW[:, :], "lW")
+        if last: quant(T.qv[:, :], T.sv_[:, :], T.vb[:, :], ["vb"], ["qv"])
+        else:
+            tt(col("ta0", 1), sm("iotaT"), sm("dT"), A.subtract, ["iotaT", "dT"], ["ta0"])
+            cp(col("tcb", 1), sm("dT"), ["dT"], ["tcb"])
+        for k, (lo, hi) in enumerate(CH):
+            far = min(hi, F)
+            n = far - lo
+            for b in range(4):
+                mm(T[("ph", "pd")[k]][:, 512 * b:512 * b + n], T.qe[:, 128 * b:128 * b + 128], T.se_[:, 128 * b:128 * b + 128], T["ql%d" % r][:, lo:far], T["sl%d" % r][:, lo:far],
+                   ["qe%d" % b, "ql%d.%d" % (r, k), "sl%d.%d" % (r, k)], ["P" + "hd"[k] + str(b)])
+            for b in range(4):
+                src, dst, pk_ = T[("ph", "pd")[k]][:, 512 * b:512 * b + n], T.jp[:, C * b + lo:C * b + far], "P" + "hd"[k] + str(b)
+                if k == 0 or b % 2: act(dst, src, [pk_], ["jp%d%d" % (b, k)])
+                else: cp(dst, src, [pk_], ["jp%d%d" % (b, k)])
+        for t in range(4):
+            tt(T[XN][:, t:4 * C:4], T.jp[:, C * t:C * t + C].indirect(T.lW[:, :]), T[X][:, t:4 * C:4], A.add,
+               ["jp%d0" % t, "jp%d1" % t, "jp%dh" % t, "lW", X], [XN])
+
+    quant(T.qx[:, :], T.sx[:, :], T.x3[:, :], ["x3"], ["qx"])
+    dma("y", "st1", T.oc[:, :], T.qx[:, :].bitcast(dt.uint8), ["qx"], [])
+    mm(T.pd[:, 0:C], T.qv[:, :], T.sv_[:, :], T.qx[:, :], T.sx[:, :], ["qv", "qx"], ["Pd0"])
+    for k in range(4): dma("y", "st%d" % (2 + k), T.osc[4 * k:4 * k + 4, :], T.sx[32 * k:32 * k + 4, :], ["qx"], [])
+    act(T.ysb[:, :], T.pd[:, 0:C], ["Pd0"], ["ysb"])
+    dma("s", "st6", T.y[:, :], T.ysb[:, :], ["ysb"], [])
+    for s in sorted(count): wait("g", (s, count[s]))

@@ -1,21 +1,23 @@
-from concourse.bass import DstId, RemoteDMATransfer
 from concourse.mybir import dt, AluOpType, ActivationFunctionType
 
 C, F, ROUNDS = 448, 336, 3
 K = C // 16
 MASKS = [1, 2, 3]
-CH = [(0, 192), (192, 448)]
+CH = [(0, 192), (192, 336)]
+CHZ = [(0, 192), (192, 352), (352, 448)]
+OWN = (320, 448)
 NB = 1 << 9
 NK = 1 << 19
-SLOTS = ["iotaT", "mask", "inv", "dT", "nT", "C0", "h", "P", "hp", "pk", "V1", "U", "V1b", "Ub", "df", "dfo", "eo",
-         "glo", "par", "wd", "wn"] + ["A%d" % i for i in range(1, 6)] + ["B%d" % i for i in range(1, 6)]
+SLOTS = ["iotaT", "mask", "inv", "dT", "nT", "i512", "nd", "P", "hp", "pk", "pk2", "V1", "U", "V1b", "Ub", "df", "dfo", "eo",
+         "glo", "par", "wd", "wn"]
 ISLOTS = ["W", "i1", "i2", "is", "odd", "ip", "ib", "dli", "nli"]
+OPT = {"scat": 2, "z3": 1, "can": 6, "ssend": 1, "exp": 3, "pl": 0}
 
 SCRATCH = {
     "sm": ("sbuf", [128, K * len(SLOTS)], "float32"),
     "si": ("sbuf", [128, K * len(ISLOTS)], "int32"),
     "xp": ("sbuf", [128, 4 * C], "bfloat16"), "tmp": ("sbuf", [128, 4 * C], "bfloat16"),
-    "z": ("sbuf", [128, 4 * C], "bfloat16"), "hh": ("sbuf", [128, 4 * C], "bfloat16"),
+    "z": ("sbuf", [128, 4 * C], "bfloat16"), "hh": ("sbuf", [128, 4 * F], "bfloat16"),
     "jp": ("sbuf", [128, 4 * C], "bfloat16"),
     "ub": ("sbuf", [128, 512], "bfloat16"), "vb": ("sbuf", [128, 512], "bfloat16"),
     "one": ("sbuf", [128, 512], "bfloat16"),
@@ -23,25 +25,23 @@ SCRATCH = {
     "qv": ("sbuf", [128, 128], "float8_e4m3fn_x4"), "sv_": ("sbuf", [128, 128], "uint8"),
     "qx": ("sbuf", [128, C], "float8_e4m3fn_x4"), "sx": ("sbuf", [128, C], "uint8"),
     "qz": ("sbuf", [128, C], "float8_e4m3fn_x4"), "sz": ("sbuf", [128, C], "uint8"),
+    "qo": ("sbuf", [128, 128], "float8_e4m3fn_x4"), "so": ("sbuf", [128, 128], "uint8"),
     "qw": ("sbuf", [128, 512], "float8_e4m3fn_x4"), "sw": ("sbuf", [128, 512], "uint8"),
     "qe": ("sbuf", [128, 512], "float8_e4m3fn_x4"), "se_": ("sbuf", [128, 512], "uint8"),
+    "bm": ("sbuf", [128, 6 * K], "float32"), "pp": ("sbuf", [128, 6 * K], "float32"),
+    "hw": ("sbuf", [128, 6 * K], "float32"), "hpw": ("sbuf", [128, 6 * K], "float32"), "x84": ("sbuf", [128, 3 * K], "float32"),
     "ysb": ("sbuf", [128, C], "float32"),
-    "iotaS": ("sbuf", [128, C], "float32"), "nS": ("sbuf", [128, C], "float32"), "neS": ("sbuf", [128, C], "float32"),
-    "einv": ("sbuf", [128, C], "float32"), "m16": ("sbuf", [128, C], "float32"), "rst": ("sbuf", [128, C], "float32"),
-    "c16": ("sbuf", [128, C], "float32"), "gm": ("sbuf", [128, C], "float32"), "sc": ("sbuf", [128, C], "float32"),
-    "ts": ("sbuf", [128, C], "float32"), "tbb": ("sbuf", [128, C], "float32"), "tcb": ("sbuf", [128, C], "float32"),
-    "tfb": ("sbuf", [128, C], "float32"), "sg": ("sbuf", [128, C], "float32"), "te": ("sbuf", [128, C], "float32"),
-    "s480": ("sbuf", [128, C + 32], "float32"), "t480": ("sbuf", [128, C + 32], "float32"),
-    "r480": ("sbuf", [128, C + 32], "float32"), "f480": ("sbuf", [128, C + 32], "float32"),
     "ph": ("psum", [128, 2048], "float32"), "pd": ("psum", [128, 2048], "float32"),
-    "pq": ("sbuf", [128, 1], "float32"), "pi": ("sbuf", [128, 1], "int32"),
+    "pq": ("sbuf", [128, 1], "float32"),
 }
+for _n in ("iotaS", "einv", "m16", "rst", "c16", "gm", "sc", "ta0", "ca", "can", "tac", "ts", "tbb", "tcb", "tfb", "spk", "te", "tm", "mi"):
+    SCRATCH[_n] = ("sbuf", [128, C], "float32")
+for _n in ("s480", "t480", "r480", "f480"): SCRATCH[_n] = ("sbuf", [128, C + 32], "float32")
 for _n in ("dW", "nW", "eW", "pW", "aW", "bW", "lW"): SCRATCH[_n] = ("sbuf", [128, K], "uint16")
 for _i in range(4):
     SCRATCH["x%d" % _i] = ("sbuf", [128, 4 * C], "bfloat16")
     SCRATCH["et%d" % _i] = ("sbuf", [128, 512], "bfloat16")
 for _i in range(6):
-    SCRATCH["ta%d" % _i] = ("sbuf", [128, C], "float32")
     SCRATCH["tb%d" % _i] = ("sbuf", [128, C], "float32")
     SCRATCH["sa%d" % _i] = ("sbuf", [128, C], "float32")
 for _i in range(7): SCRATCH["sb%d" % _i] = ("sbuf", [128, C], "float32")
@@ -55,7 +55,7 @@ for _r in range(ROUNDS):
     SCRATCH["ql%d" % _r] = ("sbuf", [128, F], "float8_e4m3fn_x4")
     SCRATCH["sl%d" % _r] = ("sbuf", [128, F], "uint8")
 
-SEMAPHORES = ["qv", "qs", "qt", "qg"] + ["ld%d" % i for i in range(9)] + ["st%d" % i for i in range(7)]
+SEMAPHORES = ["qv", "qs", "qt", "qg", "da"] + ["ld%d" % i for i in range(9)] + ["st%d" % i for i in range(7)]
 for _r in range(ROUNDS):
     for _n in ("t", "l", "c0", "s0", "c1", "s1"): SEMAPHORES += ["a%s%d" % (_n, _r), "o%s%d" % (_n, _r)]
 
@@ -81,15 +81,13 @@ def rank_program(g, core, T, topo):
     def need(q, r, w):
         deps = []
         for k in r: deps += lastw.get(k, [])
-        for k in w:
-            deps += lastw.get(k, [])
-            deps += readers.get(k, [])
+        for k in w: deps += lastw.get(k, []) + readers.get(k, [])
         best = {}
         for s, n in deps: best[s] = max(n, best.get(s, 0))
         for s in sorted(best): wait(q, (s, best[s]))
 
     def done(q, ev, r, w):
-        if q: snap[ev] = dict(known[q])
+        snap[ev] = dict(known[q])
         for k in r: readers.setdefault(k, []).append(ev)
         for k in w: lastw[k], readers[k] = [ev], []
 
@@ -105,8 +103,8 @@ def rank_program(g, core, T, topo):
     def dma(q, sem, out, in_, r, w):
         need(q, r, w)
         eng[q].dma_start(out, in_).then_inc(T.sem[sem], 16)
-        count[sem] = 16
-        done(q, (sem, 16), r, w)
+        count[sem] = count.get(sem, 0) + 16
+        done(q, (sem, count[sem]), r, w)
 
     def send(dst, name, out, in_, r):
         need("g", r, [])
@@ -127,6 +125,8 @@ def rank_program(g, core, T, topo):
     def si(n):
         i = ISLOTS.index(n)
         return T.si[:, K * i:K * i + K]
+
+    def sl(b, i, n=1): return T[b][:, K * i:K * i + K * n]
 
     def col(b, q):
         return T[b][:, q:C:16]
@@ -149,6 +149,8 @@ def rank_program(g, core, T, topo):
         if f: op("g", lambda: g.iota(out, pat, base, cm, allow_small_or_imprecise_dtypes=True), [], w)
         else: op("g", lambda: g.iota(out, pat, base, cm), [], w)
 
+    def zero(ap, w): iota(ap, [[0, ap.shape[1]]], 0, 0, w)
+
     peer = [T.cores[rank ^ m] for m in MASKS]
     for r in range(ROUNDS):
         arrives(peer[r], "t%d" % r, ["tland%d" % r])
@@ -170,13 +172,9 @@ def rank_program(g, core, T, topo):
     iota(si("ip"), [[0, K]], 0, 1, ["ip"], False)
     iota(sm("glo"), [[0, K // 2], [1, 2]], 0, 0, ["glo"])
     iota(si("ib"), [[32, K // 2], [0, 2]], 0, 0, ["ib"], False)
-    iota(T.iotaS[:, :], [[1, C]], 0, 0, ["iotaS"])
-    iota(T.c16[:, :], [[0, K], [1, 16]], 0, 0, ["c16"])
-    for b in ("ta0", "tbb", "tcb", "tfb"): fill(T[b][:, :], 0.0, [b])
-    for b in ("s480", "r480"): fill(T[b][:, :], 0.0, [b])
-    fill(T.one[:, :], 1.0, ["one"])
-    for b in range(4):
-        op("g", lambda: g.affine_select(T["et%d" % b][:, :], T.one[:, :], [[-1, 512]], A.is_equal, 0.0, b, 4), ["one"], ["et%d" % b])
+    zero(T.ta0[:, :], ["ta0"])
+    zero(T.tbb[:, :], ["tbb"])
+    for b in ("tfb", "r480"): fill(T[b][:, :], 0.0, [b])
     ts2(si("i1"), si("ip"), 4, A.arith_shift_right, 1, A.bitwise_and, ["ip"], ["i1"])
     cp(sm("par"), si("i1"), ["i1"], ["par"])
     tt(sm("mask"), sm("par"), sm("glo"), A.is_equal, ["par", "glo"], ["mask"])
@@ -200,138 +198,185 @@ def rank_program(g, core, T, topo):
     swap("tfb", "r480", "f480", [(T.lsend0[:, K:2 * K], ["ls0w"]), (sm("wn"), ["wn"])], [(sm("dT"), ["dT"]), (sm("nT"), ["nT"])])
     cp(T.lsend0[:, 0:K], sm("dT"), ["dT"], ["ls0t"])
     send(peer[0], "l0", T.lland0[:, :], T.lsend0[:, :], ["ls0w", "ls0t"])
-    ts2(sm("h"), sm("nT"), float(NB), A.mult, 0.0, A.add, ["nT"], ["h"])
-    tt(sm("C0"), sm("h"), sm("iotaT"), A.add, ["h", "iotaT"], ["C0"])
-    tt(col("ta0", 1), sm("iotaT"), sm("dT"), A.subtract, ["iotaT", "dT"], ["ta0"])
-    cp(col("tcb", 1), sm("dT"), ["dT"], ["tcb"])
-    ts1(si("i1"), si("ip"), 15, A.bitwise_and, ["ip"], ["i1"])
-    cp(T.pq[:, :], T.si[:, K * ISLOTS.index("i1"):K * ISLOTS.index("i1") + 1], ["i1"], ["pq"])
-    ts1(T.m16[:, :], T.c16[:, :], T.pq[:, :], A.is_equal, ["c16", "pq"], ["m16"])
-    ts1(T.rst[:, :], T.c16[:, :], 0.0, A.not_equal, ["c16"], ["rst"])
-    act(T.nS[:, :], T.iotaS[:, :].indirect(T.nW[:, :]), ["iotaS", "nW"], ["nS"])
     quant(T.qu[:, :], T.su[:, :], T.ub[:, :], ["ub"], ["qu"])
+    zero(T.ca[:, :], ["ca%d" % i for i in range(7)])
+    zero(T.tcb[:, :], ["tcb"])
+    cp(col("ta0", 4), sm("iotaT"), ["iotaT"], ["ta0"])
+    fill(T.tm[:, :], 1e29, ["tm"])
 
-    def to_table(win, off, wkeys, out, okey):
+    def late_constants():
+        zero(T.s480[:, :], ["s480"])
+        iota(T.iotaS[:, :], [[1, C]], 0, 0, ["iotaS"])
+        iota(T.c16[:, :], [[0, K], [1, 16]], 0, 0, ["c16"])
+        fill(T.one[:, :], 1.0, ["one"])
+        for b in range(4):
+            op("g", lambda: g.affine_select(T["et%d" % b][:, :], T.one[:, :], [[-1, 512]], A.is_equal, 0.0, b, 4), ["one"], ["et%d" % b])
+        ts1(sm("i512"), sm("iotaT"), float(NB), A.mult, ["iotaT"], ["i512"])
+        ts1(si("i1"), si("ip"), 15, A.bitwise_and, ["ip"], ["i1"])
+        cp(T.pq[:, :], T.si[:, K * ISLOTS.index("i1"):K * ISLOTS.index("i1") + 1], ["i1"], ["pq"])
+        ts1(T.m16[:, :], T.c16[:, :], T.pq[:, :], A.is_equal, ["c16", "pq"], ["m16"])
+        ts1(T.rst[:, :], T.c16[:, :], 0.0, A.not_equal, ["c16"], ["rst"])
+
+    def pick16(win, off, wkeys):
         tt(T.gm[:, :], win.indirect(off), T.m16[:, :], A.mult, wkeys + ["m16"], ["gm"])
+
+    def fold16(out, okey):
         op("v", lambda: g.vector.tensor_tensor_scan(T.sc[:, :], T.rst[:, :], T.gm[:, :], 0.0, A.mult, A.add), ["rst", "gm"], ["sc"])
         cp(out, T.sc[:, 15:C:16], ["sc"], [okey])
+
+    def partner_list(r):
+        cp(T.eW[:, :], T["lland%d" % r][:, K:2 * K], ["lland%d" % r], ["eW"])
+        tt(sm("eo"), T["lland%d" % r][:, 0:K], sm("iotaT"), A.subtract, ["lland%d" % r, "iotaT"], ["eo"])
+        ts2(col("tbb", 8), sm("eo"), float(NB), A.mult, float(NK), A.add, ["eo"], ["tbb"])
+
+    def invert(): op("v", lambda: g.vector.tensor_copy(T.einv[:, :].indirect(T.eW[:, :]), T.iotaS[:, :]), ["eW", "iotaS"], ["einv"])
 
     for r in range(ROUNDS):
         p = peer[r]
         X, XN = "x%d" % r, "x%d" % (r + 1)
+        ll, lk = T["lland%d" % r], "lland%d" % r
         quant(T.qx[:, :], T.sx[:, :], T[X][:, :], [X], ["qx"])
         mm(T.pd[:, 0:C], T.qu[:, :], T.su[:, :], T.qx[:, :], T.sx[:, :], ["qu", "qx"], ["Pd0"])
+        tt(col("ta0", 8), sm("iotaT"), sm("dT"), A.subtract, ["iotaT", "dT"], ["ta0"])
+        tt(sm("nd"), sm("nT"), sm("dT"), A.subtract, ["nT", "dT"], ["nd"])
+        if r: partner_list(r)
+        if OPT["scat"] == 4: invert()
         for t in range(4): act(T.xp[:, C * t:C * t + C], T[X][:, t:4 * C:4], [X], ["xp%d" % t], 0.5)
-        if r == 0:
-            for b in range(4): quant(T.qe[:, 128 * b:128 * b + 128], T.se_[:, 128 * b:128 * b + 128], T["et%d" % b][:, :], ["et%d" % b], ["qe%d" % b])
         tr(T.ts[:, :], T.pd[:, 0:C], ["Pd0"], ["ts"])
-        cp(T["tsend%d" % r][:, :], col("ts", 0), ["ts"], ["tsend%d" % r])
+        if OPT["ssend"]: act(T["tsend%d" % r][:, :], col("ts", 0), ["ts"], ["tsend%d" % r])
+        else: cp(T["tsend%d" % r][:, :], col("ts", 0), ["ts"], ["tsend%d" % r])
         send(p, "t%d" % r, T["tland%d" % r][:, :], T["tsend%d" % r][:, :], ["tsend%d" % r])
         cp(col("ta0", 0), col("ts", 0), ["ts"], ["ta0"])
+        cp(col("tm", 0), col("ts", 0), ["ts"], ["tm"])
         tr(T.sa0[:, :], T.ta0[:, :], ["ta0"], ["sa0"])
-        ll = T["lland%d" % r]
-        lk = "lland%d" % r
+        tr(T.mi[:, :], T.tm[:, :], ["tm"], ["mi"])
 
-        def chain_a(i):
-            act(T["sa%d" % i][:, :], T["sa%d" % (i - 1)][:, :].indirect(T.dW[:, :]), ["sa%d" % (i - 1), "dW"], ["sa%d" % i])
-        chain_a(1)
-        chain_a(2)
-        tt(sm("pk"), sm("C0"), col("ta0", 1), A.subtract, ["C0", "ta0"], ["pk"])
+        def rows(i): dma("y", "da", T.ca[i:128:8, :], T["sa%d" % i][0:128:8, :], ["sa%d" % i], ["ca%d" % i])
+        rows(0)
+        for i in range(1, 6):
+            if i == OPT["exp"]:
+                if r == 0: partner_list(0)
+                cp(col("tbb", 0), T["tland%d" % r][:, :], ["tland%d" % r], ["tbb"])
+                tr(T.sb0[:, :], T.tbb[:, :], ["tbb"], ["sb0"])
+            tt(T["sa%d" % i][:, :], T["sa%d" % (i - 1)][:, :].indirect(T.dW[:, :]), T.mi[:, :], A.min, ["sa%d" % (i - 1), "dW", "mi"], ["sa%d" % i])
+            rows(i)
+        dma("y", "da", T.ca[6:128:16, :], T.sa5[4:128:16, :], ["sa5"], ["ca6"])
+        cp(sl("bm", 0), T["tland%d" % r][:, :], ["tland%d" % r], ["bm0"])
+        if OPT["scat"] == 1: invert()
+        for j in range(1, 6): act(T["sb%d" % j][:, :], T["sb%d" % (j - 1)][:, :].indirect(T.eW[:, :]), ["sb%d" % (j - 1), "eW"], ["sb%d" % j])
+        act(T.can[:, :], T.ca[:, :].indirect(T.nW[:, :]), ["nW"] + ["ca%d" % i for i in range(7)], ["can"])
 
-        def own_step(i):
-            tr(T["ta%d" % i][:, :], T["sa%d" % i][:, :], ["sa%d" % i], ["ta%d" % i])
-            prev, pkey = (col("ta0", 0), "ta0") if i == 1 else (sm("A%d" % (i - 1)), "A%d" % (i - 1))
-            tt(sm("A%d" % i), prev, col("ta%d" % i, 0), A.min, [pkey, "ta%d" % i], ["A%d" % i])
-            tt(sm("pk"), sm("pk"), col("ta%d" % i, 1), A.subtract, ["pk", "ta%d" % i], ["pk"])
-        own_step(1)
-        cp(T.eW[:, :], ll[:, K:2 * K], [lk], ["eW"])
-        act(T.neS[:, :], T.nS[:, :].indirect(T.eW[:, :]), ["nS", "eW"], ["neS"])
-        for i in (3, 4, 5): chain_a(i)
-        own_step(2)
-        to_table(T.neS[:, :], T.nW[:, :], ["neS", "nW"], T.pW[:, :], "pW")
-        tt(sm("eo"), ll[:, 0:K], sm("iotaT"), A.subtract, [lk, "iotaT"], ["eo"])
-        ts2(col("tbb", 1), sm("eo"), float(NB), A.mult, float(NK), A.add, ["eo"], ["tbb"])
-        own_step(3)
-        own_step(4)
-        cp(col("tbb", 0), T["tland%d" % r][:, :], ["tland%d" % r], ["tbb"])
-        tr(T.sb0[:, :], T.tbb[:, :], ["tbb"], ["sb0"])
-        act(T.sb1[:, :], T.sb0[:, :].indirect(T.nW[:, :]), ["sb0", "nW"], ["sb1"])
-        for j in range(2, 7): act(T["sb%d" % j][:, :], T["sb%d" % (j - 1)][:, :].indirect(T.pW[:, :]), ["sb%d" % (j - 1), "pW"], ["sb%d" % j])
-        own_step(5)
-        for j in range(6):
-            tb, ta = "tb%d" % j, "ta%d" % (5 - j)
-            tr(T[tb][:, :], T["sb%d" % (j + 1)][:, :], ["sb%d" % (j + 1)], [tb])
-            tt(sm("P"), col(tb, 1), col(ta, 1), A.add, [tb, ta], ["P"])
-            if j == 0: bm, bk = col(tb, 0), tb
-            else:
-                pm, pmk = (col("tb0", 0), "tb0") if j == 1 else (sm("B%d" % (j - 1)), "B%d" % (j - 1))
-                bm, bk = sm("B%d" % j), "B%d" % j
-                tt(bm, pm, col(tb, 0), A.min, [pmk, tb], [bk])
-            am, ak = (col("ta0", 0), "ta0") if j == 5 else (sm("A%d" % (5 - j)), "A%d" % (5 - j))
-            tt(sm("h"), am, bm, A.is_le, [ak, bk], ["h"])
-            tt(sm("hp"), sm("h"), sm("P"), A.mult, ["h", "P"], ["hp"])
-            if j < 5: tt(sm("pk"), sm("pk"), sm("hp"), A.add, ["pk", "hp"], ["pk"])
-            else: tt(col("tcb", 0), sm("pk"), sm("hp"), A.add, ["pk", "hp"], ["tcb"])
-        tr(T.s480[:, 16:16 + C], T.tcb[:, :], ["tcb"], ["s480"])
-        tt(sm("V1"), col("tcb", 0), sm("mask"), A.mult, ["tcb", "mask"], ["V1"])
+        def tb_(j): tr(T["tb%d" % j][:, :], T["sb%d" % j][:, :], ["sb%d" % j], ["tb%d" % j])
+        def bm_(j): tt(sl("bm", j), sl("bm", j - 1), col("tb%d" % j, 0), A.min, ["bm%d" % (j - 1), "tb%d" % j], ["bm%d" % j])
+        def pp_(j):
+            b = "tb%d" % j if j else "tbb"
+            tt(sl("pp", j), col(b, 8), col("tac", 13 - j), A.add, [b, "tac"], ["pp%d" % j])
+        def h_(j): tt(sl("hw", j), col("tac", 5 - j), sl("bm", j), A.is_le, ["tac", "bm%d" % j], ["hw%d" % j])
+        if r == 0: late_constants()
+        for j in range(1, OPT["can"]): tb_(j)
+        for j in range(1, OPT["can"]): bm_(j)
+        if OPT["scat"] == 0: invert()
+        tr(T.tac[:, :], T.can[:, :], ["can"], ["tac"])
+        tt(sm("pk"), sm("i512"), col("tac", 6), A.add, ["i512", "tac"], ["pk"])
+        for j in range(0, OPT["can"]):
+            pp_(j)
+            h_(j)
+        tt(sm("pk2"), sm("pk"), col("tac", 13), A.subtract, ["pk", "tac"], ["pk2"])
+        for j in range(OPT["can"], 6):
+            tb_(j)
+            bm_(j)
+            pp_(j)
+            h_(j)
+        tt(T.hpw[:, :], T.hw[:, :], T.pp[:, :], A.mult, ["%s%d" % (b, j) for b in ("hw", "pp") for j in range(6)], ["hpw"])
+        tt(T.x84[:, :], sl("hpw", 0, 3), sl("hpw", 3, 3), A.add, ["hpw"], ["x84"])
+        tt(sm("P"), sl("x84", 0), sl("x84", 1), A.add, ["x84"], ["P"])
+        tt(sm("hp"), sl("x84", 2), sm("pk2"), A.add, ["x84", "pk2"], ["hp"])
+        tt(col("tcb", 0), sm("P"), sm("hp"), A.add, ["P", "hp"], ["tcb"])
+        tr(T.spk[:, :], T.tcb[:, :], ["tcb"], ["spk"])
+        act(T.s480[:, 16:16 + C], T.spk[:, :].indirect(T.nW[:, :]), ["spk", "nW"], ["s480"])
+        if OPT["scat"] == 2: invert()
+        tr(T.te[:, :], T.s480[:, 16:16 + C], ["s480"], ["te"])
         tr(T.t480[:, :], T.s480[:, :], ["s480"], ["t480"])
+        tt(sm("V1"), col("te", 0), sm("mask"), A.mult, ["te", "mask"], ["V1"])
         tt(sm("U"), shifted("t480", 0), sm("inv"), A.mult, ["t480", "inv"], ["U"])
         tt(si("W"), sm("V1"), sm("U"), A.add, ["V1", "U"], ["W"])
         ts1(si("i1"), si("W"), NB - 1, A.bitwise_and, ["W"], ["i1"])
         cp(T.aW[:, :], si("i1"), ["i1"], ["aW"])
         ts2(si("i2"), si("W"), 9, A.arith_shift_right, NB - 1, A.bitwise_and, ["W"], ["i2"])
         cp(T.bW[:, :], si("i2"), ["i2"], ["bW"])
-        for k, (lo, hi) in enumerate(CH):
-            n = hi - lo
-            for t in range(4):
-                win = T.xp[:, C * t:C * t + C]
-                tmp, tk = T.tmp[:, C * t + lo:C * t + hi], "tmp%d%d" % (k, t)
-                act(tmp, win.indirect(T.aW[:, lo // 16:hi // 16]), ["xp%d" % t, "aW"], [tk])
-                tt(T.z[:, 4 * lo + t:4 * hi:4], win.indirect(T.bW[:, lo // 16:hi // 16]), tmp, A.add, ["xp%d" % t, "bW", tk], ["z%d" % k])
-            quant(T.qz[:, lo:hi], T.sz[:, lo:hi], T.z[:, 4 * lo:4 * hi], ["z%d" % k], ["qz%d" % k])
+
+        def gather_a(k, t):
+            lo, hi = CHZ[k]
+            act(T.tmp[:, C * t + lo:C * t + hi], T.xp[:, C * t:C * t + C].indirect(T.aW[:, lo // 16:hi // 16]), ["xp%d" % t, "aW"], ["tmp%d%d" % (k, t)])
+
+        def add_b(k, t):
+            lo, hi = CHZ[k]
+            tt(T.z[:, 4 * lo + t:4 * hi:4], T.xp[:, C * t:C * t + C].indirect(T.bW[:, lo // 16:hi // 16]), T.tmp[:, C * t + lo:C * t + hi], A.add,
+               ["xp%d" % t, "bW", "tmp%d%d" % (k, t)], ["z%d%d" % (k, t)])
+
+        def layer(lo, hi, bank, q, s, c0, zk, qk):
+            quant(T[q][:, lo - c0:hi - c0], T[s][:, lo - c0:hi - c0], T.z[:, 4 * lo:4 * hi], ["z%d%d" % (k, t) for k in zk for t in range(4)], [qk])
             for i in range(4):
-                mm(T[("ph", "pd")[k]][:, 512 * i:512 * i + n], T.qw[:, 128 * i:128 * i + 128], T.sw[:, 128 * i:128 * i + 128], T.qz[:, lo:hi], T.sz[:, lo:hi],
-                   ["qw", "sw", "qz%d" % k], ["P" + "hd"[k] + str(i)])
-        for k, (lo, hi) in enumerate(CH):
-            n, far = hi - lo, min(hi, F)
-            for i in range(4):
-                src, dst, pk_ = T[("ph", "pd")[k]][:, 512 * i:512 * i + n], T.hh[:, 4 * lo + i:4 * hi:4], "P" + "hd"[k] + str(i)
-                if k == 0 or i % 2: act(dst, src, [pk_], ["hh%d%d" % (k, i)], 0.03125)
-                else: ts1(dst, src, 0.03125, A.mult, [pk_], ["hh%d%d" % (k, i)])
-            quant(T["qh%d" % r][:, lo:far], T["sh%d" % r][:, lo:far], T.hh[:, 4 * lo:4 * far], ["hh%d%d" % (k, i) for i in range(4)], ["qh%d%d" % (r, k)])
-            send(p, "c%d%d" % (k, r), T["ql%d" % r][:, lo:far].bitcast(dt.uint8), T["qh%d" % r][:, lo:far].bitcast(dt.uint8), ["qh%d%d" % (r, k)])
-            send(p, "s%d%d" % (k, r), T["sl%d" % r][:, lo:far], T["sh%d" % r][:, lo:far], ["qh%d%d" % (r, k)])
-        act(T.sg[:, :], T.s480[:, 16:16 + C].indirect(T.nW[:, :]), ["s480", "nW"], ["sg"])
-        for t in range(4): act(T.jp[:, C * t + F:C * t + C], T.hh[:, 4 * F + t:4 * C:4], ["hh1%d" % t], ["jp%dh" % t])
-        tr(T.te[:, :], T.sg[:, :], ["sg"], ["te"])
+                mm(T[bank][:, 512 * i:512 * i + hi - lo], T.qw[:, 128 * i:128 * i + 128], T.sw[:, 128 * i:128 * i + 128], T[q][:, lo - c0:hi - c0], T[s][:, lo - c0:hi - c0],
+                   ["qw", "sw", qk], ["P" + bank[1] + str(i)])
+
+        def pack(k):
+            lo, hi = CH[k]
+            quant(T["qh%d" % r][:, lo:hi], T["sh%d" % r][:, lo:hi], T.hh[:, 4 * lo:4 * hi], ["hh%d%d" % (k, i) for i in range(4)], ["qh%d%d" % (r, k)])
+            send(p, "c%d%d" % (k, r), T["ql%d" % r][:, lo:hi].bitcast(dt.uint8), T["qh%d" % r][:, lo:hi].bitcast(dt.uint8), ["qh%d%d" % (r, k)])
+            send(p, "s%d%d" % (k, r), T["sl%d" % r][:, lo:hi], T["sh%d" % r][:, lo:hi], ["qh%d%d" % (r, k)])
+
+        def evac(k, i, q):
+            lo, hi = CH[k]
+            src, dst, pk_ = T[("ph", "pd")[k]][:, 512 * i:512 * i + hi - lo], T.hh[:, 4 * lo + i:4 * hi:4], "P" + "hd"[k] + str(i)
+            if q == "s": act(dst, src, [pk_], ["hh%d%d" % (k, i)], 0.03125)
+            else: ts1(dst, src, 0.03125, A.mult, [pk_], ["hh%d%d" % (k, i)])
+
+        for k in range(2):
+            for t in range(4): gather_a(k, t)
+        for t in range(4): add_b(0, t)
+        layer(0, 192, "ph", "qz", "sz", 0, [0], "qz0")
+        for t in range(4): add_b(1, t)
+        layer(192, 336, "pd", "qz", "sz", 0, [1], "qz1")
+        for i in range(4): evac(0, i, "s")
+        pack(0)
+        for i in range(4): evac(1, i, "vs"[i % 2])
+        for t in range(4): gather_a(2, t)
+        pack(1)
+
+        def own_part():
+            for t in range(4): add_b(2, t)
+            layer(OWN[0], OWN[1], "ph", "qo", "so", OWN[0], [1, 2], "qo")
+            for i in range(4): act(T.jp[:, C * i + F:C * i + C], T.ph[:, 512 * i + F - OWN[0]:512 * i + C - OWN[0]], ["Ph%d" % i], ["jp%dh" % i], 0.03125)
+        if OPT["z3"] == 1: own_part()
         tt(si("is"), col("tcb", 0), col("te", 0), A.add, ["tcb", "te"], ["is"])
+        tt(sm("df"), sm("nd"), col("tac", 8), A.subtract, ["nd", "tac"], ["df"])
         ts2(si("odd"), si("is"), 19, A.arith_shift_right, 1, A.bitwise_and, ["is"], ["odd"])
-        tt(sm("df"), col("te", 1), sm("dT"), A.subtract, ["te", "dT"], ["df"])
         tt(sm("dfo"), sm("df"), si("odd"), A.mult, ["df", "odd"], ["dfo"])
         tt(sm("dT"), sm("dT"), sm("dfo"), A.add, ["dT", "dfo"], ["dT"])
         last = r == ROUNDS - 1
         fw, fk = (sm("wd"), "wd") if last else (T["lsend%d" % (r + 1)][:, K:2 * K], "ls%dw" % (r + 1))
+        if not last: cp(T["lsend%d" % (r + 1)][:, 0:K], sm("dT"), ["dT"], ["ls%dt" % (r + 1)])
         swap("tfb", "r480", "f480", [(sm("dT"), ["dT"])], [(fw, [fk])])
         cp(T.dW[:, :], fw, [fk], ["dW"])
         if last:
             dma("y", "st0", T.dn[:, :], T.r480[0:128:16, 16:16 + C], ["r480"], [])
         else:
-            cp(T["lsend%d" % (r + 1)][:, 0:K], sm("dT"), ["dT"], ["ls%dt" % (r + 1)])
             send(peer[r + 1], "l%d" % (r + 1), T["lland%d" % (r + 1)][:, :], T["lsend%d" % (r + 1)][:, :], ["ls%dw" % (r + 1), "ls%dt" % (r + 1)])
-        op("v", lambda: g.vector.tensor_copy(T.einv[:, :].indirect(T.eW[:, :]), T.iotaS[:, :]), ["eW", "iotaS"], ["einv"])
-        to_table(T.einv[:, :], T.dW[:, :], ["einv", "dW"], T.lW[:, :], "lW")
+        if OPT["scat"] == 3: invert()
+        if OPT["z3"] == 0: own_part()
+        pick16(T.einv[:, :], T.dW[:, :], ["einv", "dW"])
+        fold16(T.lW[:, :], "lW")
+        if r == 0:
+            for b in range(4): quant(T.qe[:, 128 * b:128 * b + 128], T.se_[:, 128 * b:128 * b + 128], T["et%d" % b][:, :], ["et%d" % b], ["qe%d" % b])
         if last: quant(T.qv[:, :], T.sv_[:, :], T.vb[:, :], ["vb"], ["qv"])
-        else:
-            tt(col("ta0", 1), sm("iotaT"), sm("dT"), A.subtract, ["iotaT", "dT"], ["ta0"])
-            cp(col("tcb", 1), sm("dT"), ["dT"], ["tcb"])
         for k, (lo, hi) in enumerate(CH):
-            far = min(hi, F)
-            n = far - lo
+            n = hi - lo
             for b in range(4):
-                mm(T[("ph", "pd")[k]][:, 512 * b:512 * b + n], T.qe[:, 128 * b:128 * b + 128], T.se_[:, 128 * b:128 * b + 128], T["ql%d" % r][:, lo:far], T["sl%d" % r][:, lo:far],
+                mm(T[("ph", "pd")[k]][:, 512 * b:512 * b + n], T.qe[:, 128 * b:128 * b + 128], T.se_[:, 128 * b:128 * b + 128], T["ql%d" % r][:, lo:hi], T["sl%d" % r][:, lo:hi],
                    ["qe%d" % b, "ql%d.%d" % (r, k), "sl%d.%d" % (r, k)], ["P" + "hd"[k] + str(b)])
             for b in range(4):
-                src, dst, pk_ = T[("ph", "pd")[k]][:, 512 * b:512 * b + n], T.jp[:, C * b + lo:C * b + far], "P" + "hd"[k] + str(b)
+                src, dst, pk_ = T[("ph", "pd")[k]][:, 512 * b:512 * b + n], T.jp[:, C * b + lo:C * b + hi], "P" + "hd"[k] + str(b)
                 if k == 0 or b % 2: act(dst, src, [pk_], ["jp%d%d" % (b, k)])
                 else: cp(dst, src, [pk_], ["jp%d%d" % (b, k)])
         for t in range(4):

from concourse.mybir import dt, AluOpType, ActivationFunctionType

C, F, ROUNDS = 448, 336, 3
K = C // 16
MASKS = [1, 2, 3]
CH = [(0, 192), (192, 336)]
CHZ = [(0, 192), (192, 352), (352, 448)]
OWN = (320, 448)
NB = 1 << 9
NK = 1 << 19
SLOTS = ["iotaT", "mask", "inv", "dT", "nT", "i512", "nd", "P", "hp", "pk", "pk2", "V1", "U", "V1b", "Ub", "df", "dfo", "eo",
         "glo", "par", "wd", "wn"]
ISLOTS = ["W", "i1", "i2", "is", "odd", "ip", "ib", "dli", "nli"]
OPT = {"scat": 2, "z3": 1, "can": 6, "ssend": 1, "exp": 3, "pl": 0}

SCRATCH = {
    "sm": ("sbuf", [128, K * len(SLOTS)], "float32"),
    "si": ("sbuf", [128, K * len(ISLOTS)], "int32"),
    "xp": ("sbuf", [128, 4 * C], "bfloat16"), "tmp": ("sbuf", [128, 4 * C], "bfloat16"),
    "z": ("sbuf", [128, 4 * C], "bfloat16"), "hh": ("sbuf", [128, 4 * F], "bfloat16"),
    "jp": ("sbuf", [128, 4 * C], "bfloat16"),
    "ub": ("sbuf", [128, 512], "bfloat16"), "vb": ("sbuf", [128, 512], "bfloat16"),
    "one": ("sbuf", [128, 512], "bfloat16"),
    "qu": ("sbuf", [128, 128], "float8_e4m3fn_x4"), "su": ("sbuf", [128, 128], "uint8"),
    "qv": ("sbuf", [128, 128], "float8_e4m3fn_x4"), "sv_": ("sbuf", [128, 128], "uint8"),
    "qx": ("sbuf", [128, C], "float8_e4m3fn_x4"), "sx": ("sbuf", [128, C], "uint8"),
    "qz": ("sbuf", [128, C], "float8_e4m3fn_x4"), "sz": ("sbuf", [128, C], "uint8"),
    "qo": ("sbuf", [128, 128], "float8_e4m3fn_x4"), "so": ("sbuf", [128, 128], "uint8"),
    "qw": ("sbuf", [128, 512], "float8_e4m3fn_x4"), "sw": ("sbuf", [128, 512], "uint8"),
    "qe": ("sbuf", [128, 512], "float8_e4m3fn_x4"), "se_": ("sbuf", [128, 512], "uint8"),
    "bm": ("sbuf", [128, 6 * K], "float32"), "pp": ("sbuf", [128, 6 * K], "float32"),
    "hw": ("sbuf", [128, 6 * K], "float32"), "hpw": ("sbuf", [128, 6 * K], "float32"), "x84": ("sbuf", [128, 3 * K], "float32"),
    "ysb": ("sbuf", [128, C], "float32"),
    "ph": ("psum", [128, 2048], "float32"), "pd": ("psum", [128, 2048], "float32"),
    "pq": ("sbuf", [128, 1], "float32"),
}
for _n in ("iotaS", "einv", "m16", "rst", "c16", "gm", "sc", "ta0", "ca", "can", "tac", "ts", "tbb", "tcb", "tfb", "spk", "te", "tm", "mi"):
    SCRATCH[_n] = ("sbuf", [128, C], "float32")
for _n in ("s480", "t480", "r480", "f480"): SCRATCH[_n] = ("sbuf", [128, C + 32], "float32")
for _n in ("dW", "nW", "eW", "pW", "aW", "bW", "lW"): SCRATCH[_n] = ("sbuf", [128, K], "uint16")
for _i in range(4):
    SCRATCH["x%d" % _i] = ("sbuf", [128, 4 * C], "bfloat16")
    SCRATCH["et%d" % _i] = ("sbuf", [128, 512], "bfloat16")
for _i in range(6):
    SCRATCH["tb%d" % _i] = ("sbuf", [128, C], "float32")
    SCRATCH["sa%d" % _i] = ("sbuf", [128, C], "float32")
for _i in range(7): SCRATCH["sb%d" % _i] = ("sbuf", [128, C], "float32")
for _r in range(ROUNDS):
    SCRATCH["tsend%d" % _r] = ("sbuf", [128, K], "float32")
    SCRATCH["tland%d" % _r] = ("sbuf", [128, K], "float32")
    SCRATCH["lsend%d" % _r] = ("sbuf", [128, 2 * K], "float32")
    SCRATCH["lland%d" % _r] = ("sbuf", [128, 2 * K], "float32")
    SCRATCH["qh%d" % _r] = ("sbuf", [128, F], "float8_e4m3fn_x4")
    SCRATCH["sh%d" % _r] = ("sbuf", [128, F], "uint8")
    SCRATCH["ql%d" % _r] = ("sbuf", [128, F], "float8_e4m3fn_x4")
    SCRATCH["sl%d" % _r] = ("sbuf", [128, F], "uint8")

SEMAPHORES = ["qv", "qs", "qt", "qg", "da"] + ["ld%d" % i for i in range(9)] + ["st%d" % i for i in range(7)]
for _r in range(ROUNDS):
    for _n in ("t", "l", "c0", "s0", "c1", "s1"): SEMAPHORES += ["a%s%d" % (_n, _r), "o%s%d" % (_n, _r)]


def rank_program(g, core, T, topo):
    rank = T.rank_of(core)
    if rank is None:
        return
    A = AluOpType
    CP = ActivationFunctionType.Copy
    eng = {"v": g.vector, "s": g.scalar, "t": g.tensor, "g": g, "y": g.sync}
    own = {"v": "qv", "s": "qs", "t": "qt", "g": "qg"}
    count, known, lastw, readers, snap = {}, {q: {} for q in eng}, {}, {}, {}

    def wait(q, ev):
        s, n = ev
        if known[q].get(s, 0) >= n: return
        eng[q].wait_ge(T.sem[s], n)
        known[q][s] = n
        for a, b in snap.get(ev, {}).items():
            if known[q].get(a, 0) < b: known[q][a] = b

    def need(q, r, w):
        deps = []
        for k in r: deps += lastw.get(k, [])
        for k in w: deps += lastw.get(k, []) + readers.get(k, [])
        best = {}
        for s, n in deps: best[s] = max(n, best.get(s, 0))
        for s in sorted(best): wait(q, (s, best[s]))

    def done(q, ev, r, w):
        snap[ev] = dict(known[q])
        for k in r: readers.setdefault(k, []).append(ev)
        for k in w: lastw[k], readers[k] = [ev], []

    def op(q, call, r, w):
        w = w + [k for k in r if k[0] == "P"]
        r = [k for k in r if k[0] != "P"]
        need(q, r, w)
        s = own[q]
        count[s] = count.get(s, 0) + 1
        call().then_inc(T.sem[s], 1)
        done(q, (s, count[s]), r, w)

    def dma(q, sem, out, in_, r, w):
        need(q, r, w)
        eng[q].dma_start(out, in_).then_inc(T.sem[sem], 16)
        count[sem] = count.get(sem, 0) + 16
        done(q, (sem, count[sem]), r, w)

    def send(dst, name, out, in_, r):
        need("g", r, [])
        m = topo.mask(core, dst)
        rid, pid = topo.addr(dst)[:2]
        g.remote_dma(out, in_, T.sem["a" + name], T.sem["o" + name], pid, rid, m)
        count["o" + name] = len(topo.engines(core, dst))
        done("g", ("o" + name, count["o" + name]), r, [])

    def arrives(src, name, w):
        count["a" + name] = len(topo.engines(src, core))
        for k in w: lastw[k] = [("a" + name, count["a" + name])]

    def sm(n):
        i = SLOTS.index(n)
        return T.sm[:, K * i:K * i + K]

    def si(n):
        i = ISLOTS.index(n)
        return T.si[:, K * i:K * i + K]

    def sl(b, i, n=1): return T[b][:, K * i:K * i + K * n]

    def col(b, q):
        return T[b][:, q:C:16]

    def shifted(b, q):
        return T[b][:, 16 + q:C + q + 1:16]

    def tt(out, a, b, o, r, w): op("v", lambda: g.vector.tensor_tensor(out, a, b, o), r, w)
    def ts1(out, a, s, o, r, w): op("v", lambda: g.vector.tensor_scalar(out, a, s, None, o), r, w)
    def ts2(out, a, s, o, s2, o2, r, w): op("v", lambda: g.vector.tensor_scalar(out, a, s, s2, o, o2), r, w)
    def cp(out, a, r, w): op("v", lambda: g.vector.tensor_copy(out, a), r, w)
    def tr(out, a, r, w): op("v", lambda: g.vector.transpose(out, a), r, w)
    def act(out, a, r, w, scale=1.0):
        if scale == 1.0: op("s", lambda: g.scalar.activation(out, a, CP), r, w)
        else: op("s", lambda: g.scalar.activation(out, a, CP, scale=scale), r, w)
    def quant(q, s, t, r, w): op("v", lambda: g.vector.quantize_mx(q, s, t), r, w)
    def mm(out, a, sa, b, sb, r, w): op("t", lambda: g.tensor.matmul_mx(out, a, sa, b, sb, True, True), r, w)
    def fill(ap, v, w): op("v", lambda: g.vector.memset(ap, v), [], w)
    def iota(out, pat, base, cm, w, f=True):
        if f: op("g", lambda: g.iota(out, pat, base, cm, allow_small_or_imprecise_dtypes=True), [], w)
        else: op("g", lambda: g.iota(out, pat, base, cm), [], w)

    def zero(ap, w): iota(ap, [[0, ap.shape[1]]], 0, 0, w)

    peer = [T.cores[rank ^ m] for m in MASKS]
    for r in range(ROUNDS):
        arrives(peer[r], "t%d" % r, ["tland%d" % r])
        arrives(peer[r], "l%d" % r, ["lland%d" % r])
        for k in range(2):
            arrives(peer[r], "c%d%d" % (k, r), ["ql%d.%d" % (r, k)])
            arrives(peer[r], "s%d%d" % (k, r), ["sl%d.%d" % (r, k)])

    dma("s", "ld0", si("dli"), T.dl[:, :], [], ["dli"])
    dma("y", "ld2", T.x0[:, 0:2 * C], T.x[:, 0:2 * C], [], ["x0"])
    dma("s", "ld1", si("nli"), T.nl[:, :], [], ["nli"])
    dma("y", "ld3", T.x0[:, 2 * C:4 * C], T.x[:, 2 * C:4 * C], [], ["x0b"])
    dma("y", "ld4", T.ub[:, :], T.u[:, :], [], ["ub"])
    dma("y", "ld5", T.qw[:, :].bitcast(dt.uint8), T.wc[:, :], [], ["qw"])
    dma("y", "ld6", T.sw[:, :], T.ws[:, :], [], ["sw"])
    dma("y", "ld7", T.vb[:, :], T.v[:, :], [], ["vb"])
    lastw["x0"] = [("ld2", 16), ("ld3", 16)]

    iota(si("ip"), [[0, K]], 0, 1, ["ip"], False)
    iota(sm("glo"), [[0, K // 2], [1, 2]], 0, 0, ["glo"])
    iota(si("ib"), [[32, K // 2], [0, 2]], 0, 0, ["ib"], False)
    zero(T.ta0[:, :], ["ta0"])
    zero(T.tbb[:, :], ["tbb"])
    for b in ("tfb", "r480"): fill(T[b][:, :], 0.0, [b])
    ts2(si("i1"), si("ip"), 4, A.arith_shift_right, 1, A.bitwise_and, ["ip"], ["i1"])
    cp(sm("par"), si("i1"), ["i1"], ["par"])
    tt(sm("mask"), sm("par"), sm("glo"), A.is_equal, ["par", "glo"], ["mask"])
    tt(sm("inv"), sm("par"), sm("glo"), A.not_equal, ["par", "glo"], ["inv"])
    ts1(si("i2"), si("ip"), 31, A.bitwise_and, ["ip"], ["i2"])
    tt(sm("iotaT"), si("i2"), si("ib"), A.add, ["i2", "ib"], ["iotaT"])

    def swap(t, s, u, vals, outs):
        for q, (v, k) in enumerate(vals): cp(col(t, q), v, k, [t])
        tr(T[s][:, 16:16 + C], T[t][:, :], [t], [s])
        tr(T[u][:, :], T[s][:, :], [s], [u])
        for q, ((v, k), (o, ok)) in enumerate(zip(vals, outs)):
            tt(sm("V1b"), v, sm("mask"), A.mult, k + ["mask"], ["V1b"])
            tt(sm("Ub"), shifted(u, q), sm("inv"), A.mult, [u, "inv"], ["Ub"])
            tt(o, sm("V1b"), sm("Ub"), A.add, ["V1b", "Ub"], ok)

    cp(T.dW[:, :], si("dli"), ["dli"], ["dW"])
    cp(T.lsend0[:, K:2 * K], si("dli"), ["dli"], ["ls0w"])
    cp(T.nW[:, :], si("nli"), ["nli"], ["nW"])
    cp(sm("wn"), si("nli"), ["nli"], ["wn"])
    swap("tfb", "r480", "f480", [(T.lsend0[:, K:2 * K], ["ls0w"]), (sm("wn"), ["wn"])], [(sm("dT"), ["dT"]), (sm("nT"), ["nT"])])
    cp(T.lsend0[:, 0:K], sm("dT"), ["dT"], ["ls0t"])
    send(peer[0], "l0", T.lland0[:, :], T.lsend0[:, :], ["ls0w", "ls0t"])
    quant(T.qu[:, :], T.su[:, :], T.ub[:, :], ["ub"], ["qu"])
    zero(T.ca[:, :], ["ca%d" % i for i in range(7)])
    zero(T.tcb[:, :], ["tcb"])
    cp(col("ta0", 4), sm("iotaT"), ["iotaT"], ["ta0"])
    fill(T.tm[:, :], 1e29, ["tm"])

    def late_constants():
        zero(T.s480[:, :], ["s480"])
        iota(T.iotaS[:, :], [[1, C]], 0, 0, ["iotaS"])
        iota(T.c16[:, :], [[0, K], [1, 16]], 0, 0, ["c16"])
        fill(T.one[:, :], 1.0, ["one"])
        for b in range(4):
            op("g", lambda: g.affine_select(T["et%d" % b][:, :], T.one[:, :], [[-1, 512]], A.is_equal, 0.0, b, 4), ["one"], ["et%d" % b])
        ts1(sm("i512"), sm("iotaT"), float(NB), A.mult, ["iotaT"], ["i512"])
        ts1(si("i1"), si("ip"), 15, A.bitwise_and, ["ip"], ["i1"])
        cp(T.pq[:, :], T.si[:, K * ISLOTS.index("i1"):K * ISLOTS.index("i1") + 1], ["i1"], ["pq"])
        ts1(T.m16[:, :], T.c16[:, :], T.pq[:, :], A.is_equal, ["c16", "pq"], ["m16"])
        ts1(T.rst[:, :], T.c16[:, :], 0.0, A.not_equal, ["c16"], ["rst"])

    def pick16(win, off, wkeys):
        tt(T.gm[:, :], win.indirect(off), T.m16[:, :], A.mult, wkeys + ["m16"], ["gm"])

    def fold16(out, okey):
        op("v", lambda: g.vector.tensor_tensor_scan(T.sc[:, :], T.rst[:, :], T.gm[:, :], 0.0, A.mult, A.add), ["rst", "gm"], ["sc"])
        cp(out, T.sc[:, 15:C:16], ["sc"], [okey])

    def partner_list(r):
        cp(T.eW[:, :], T["lland%d" % r][:, K:2 * K], ["lland%d" % r], ["eW"])
        tt(sm("eo"), T["lland%d" % r][:, 0:K], sm("iotaT"), A.subtract, ["lland%d" % r, "iotaT"], ["eo"])
        ts2(col("tbb", 8), sm("eo"), float(NB), A.mult, float(NK), A.add, ["eo"], ["tbb"])

    def invert(): op("v", lambda: g.vector.tensor_copy(T.einv[:, :].indirect(T.eW[:, :]), T.iotaS[:, :]), ["eW", "iotaS"], ["einv"])

    for r in range(ROUNDS):
        p = peer[r]
        X, XN = "x%d" % r, "x%d" % (r + 1)
        ll, lk = T["lland%d" % r], "lland%d" % r
        quant(T.qx[:, :], T.sx[:, :], T[X][:, :], [X], ["qx"])
        mm(T.pd[:, 0:C], T.qu[:, :], T.su[:, :], T.qx[:, :], T.sx[:, :], ["qu", "qx"], ["Pd0"])
        tt(col("ta0", 8), sm("iotaT"), sm("dT"), A.subtract, ["iotaT", "dT"], ["ta0"])
        tt(sm("nd"), sm("nT"), sm("dT"), A.subtract, ["nT", "dT"], ["nd"])
        if r: partner_list(r)
        if OPT["scat"] == 4: invert()
        for t in range(4): act(T.xp[:, C * t:C * t + C], T[X][:, t:4 * C:4], [X], ["xp%d" % t], 0.5)
        tr(T.ts[:, :], T.pd[:, 0:C], ["Pd0"], ["ts"])
        if OPT["ssend"]: act(T["tsend%d" % r][:, :], col("ts", 0), ["ts"], ["tsend%d" % r])
        else: cp(T["tsend%d" % r][:, :], col("ts", 0), ["ts"], ["tsend%d" % r])
        send(p, "t%d" % r, T["tland%d" % r][:, :], T["tsend%d" % r][:, :], ["tsend%d" % r])
        cp(col("ta0", 0), col("ts", 0), ["ts"], ["ta0"])
        cp(col("tm", 0), col("ts", 0), ["ts"], ["tm"])
        tr(T.sa0[:, :], T.ta0[:, :], ["ta0"], ["sa0"])
        tr(T.mi[:, :], T.tm[:, :], ["tm"], ["mi"])

        def rows(i): dma("y", "da", T.ca[i:128:8, :], T["sa%d" % i][0:128:8, :], ["sa%d" % i], ["ca%d" % i])
        rows(0)
        for i in range(1, 6):
            if i == OPT["exp"]:
                if r == 0: partner_list(0)
                cp(col("tbb", 0), T["tland%d" % r][:, :], ["tland%d" % r], ["tbb"])
                tr(T.sb0[:, :], T.tbb[:, :], ["tbb"], ["sb0"])
            tt(T["sa%d" % i][:, :], T["sa%d" % (i - 1)][:, :].indirect(T.dW[:, :]), T.mi[:, :], A.min, ["sa%d" % (i - 1), "dW", "mi"], ["sa%d" % i])
            rows(i)
        dma("y", "da", T.ca[6:128:16, :], T.sa5[4:128:16, :], ["sa5"], ["ca6"])
        cp(sl("bm", 0), T["tland%d" % r][:, :], ["tland%d" % r], ["bm0"])
        if OPT["scat"] == 1: invert()
        for j in range(1, 6): act(T["sb%d" % j][:, :], T["sb%d" % (j - 1)][:, :].indirect(T.eW[:, :]), ["sb%d" % (j - 1), "eW"], ["sb%d" % j])
        act(T.can[:, :], T.ca[:, :].indirect(T.nW[:, :]), ["nW"] + ["ca%d" % i for i in range(7)], ["can"])

        def tb_(j): tr(T["tb%d" % j][:, :], T["sb%d" % j][:, :], ["sb%d" % j], ["tb%d" % j])
        def bm_(j): tt(sl("bm", j), sl("bm", j - 1), col("tb%d" % j, 0), A.min, ["bm%d" % (j - 1), "tb%d" % j], ["bm%d" % j])
        def pp_(j):
            b = "tb%d" % j if j else "tbb"
            tt(sl("pp", j), col(b, 8), col("tac", 13 - j), A.add, [b, "tac"], ["pp%d" % j])
        def h_(j): tt(sl("hw", j), col("tac", 5 - j), sl("bm", j), A.is_le, ["tac", "bm%d" % j], ["hw%d" % j])
        if r == 0: late_constants()
        for j in range(1, OPT["can"]): tb_(j)
        for j in range(1, OPT["can"]): bm_(j)
        if OPT["scat"] == 0: invert()
        tr(T.tac[:, :], T.can[:, :], ["can"], ["tac"])
        tt(sm("pk"), sm("i512"), col("tac", 6), A.add, ["i512", "tac"], ["pk"])
        for j in range(0, OPT["can"]):
            pp_(j)
            h_(j)
        tt(sm("pk2"), sm("pk"), col("tac", 13), A.subtract, ["pk", "tac"], ["pk2"])
        for j in range(OPT["can"], 6):
            tb_(j)
            bm_(j)
            pp_(j)
            h_(j)
        tt(T.hpw[:, :], T.hw[:, :], T.pp[:, :], A.mult, ["%s%d" % (b, j) for b in ("hw", "pp") for j in range(6)], ["hpw"])
        tt(T.x84[:, :], sl("hpw", 0, 3), sl("hpw", 3, 3), A.add, ["hpw"], ["x84"])
        tt(sm("P"), sl("x84", 0), sl("x84", 1), A.add, ["x84"], ["P"])
        tt(sm("hp"), sl("x84", 2), sm("pk2"), A.add, ["x84", "pk2"], ["hp"])
        tt(col("tcb", 0), sm("P"), sm("hp"), A.add, ["P", "hp"], ["tcb"])
        tr(T.spk[:, :], T.tcb[:, :], ["tcb"], ["spk"])
        act(T.s480[:, 16:16 + C], T.spk[:, :].indirect(T.nW[:, :]), ["spk", "nW"], ["s480"])
        if OPT["scat"] == 2: invert()
        tr(T.te[:, :], T.s480[:, 16:16 + C], ["s480"], ["te"])
        tr(T.t480[:, :], T.s480[:, :], ["s480"], ["t480"])
        tt(sm("V1"), col("te", 0), sm("mask"), A.mult, ["te", "mask"], ["V1"])
        tt(sm("U"), shifted("t480", 0), sm("inv"), A.mult, ["t480", "inv"], ["U"])
        tt(si("W"), sm("V1"), sm("U"), A.add, ["V1", "U"], ["W"])
        ts1(si("i1"), si("W"), NB - 1, A.bitwise_and, ["W"], ["i1"])
        cp(T.aW[:, :], si("i1"), ["i1"], ["aW"])
        ts2(si("i2"), si("W"), 9, A.arith_shift_right, NB - 1, A.bitwise_and, ["W"], ["i2"])
        cp(T.bW[:, :], si("i2"), ["i2"], ["bW"])

        def gather_a(k, t):
            lo, hi = CHZ[k]
            act(T.tmp[:, C * t + lo:C * t + hi], T.xp[:, C * t:C * t + C].indirect(T.aW[:, lo // 16:hi // 16]), ["xp%d" % t, "aW"], ["tmp%d%d" % (k, t)])

        def add_b(k, t):
            lo, hi = CHZ[k]
            tt(T.z[:, 4 * lo + t:4 * hi:4], T.xp[:, C * t:C * t + C].indirect(T.bW[:, lo // 16:hi // 16]), T.tmp[:, C * t + lo:C * t + hi], A.add,
               ["xp%d" % t, "bW", "tmp%d%d" % (k, t)], ["z%d%d" % (k, t)])

        def layer(lo, hi, bank, q, s, c0, zk, qk):
            quant(T[q][:, lo - c0:hi - c0], T[s][:, lo - c0:hi - c0], T.z[:, 4 * lo:4 * hi], ["z%d%d" % (k, t) for k in zk for t in range(4)], [qk])
            for i in range(4):
                mm(T[bank][:, 512 * i:512 * i + hi - lo], T.qw[:, 128 * i:128 * i + 128], T.sw[:, 128 * i:128 * i + 128], T[q][:, lo - c0:hi - c0], T[s][:, lo - c0:hi - c0],
                   ["qw", "sw", qk], ["P" + bank[1] + str(i)])

        def pack(k):
            lo, hi = CH[k]
            quant(T["qh%d" % r][:, lo:hi], T["sh%d" % r][:, lo:hi], T.hh[:, 4 * lo:4 * hi], ["hh%d%d" % (k, i) for i in range(4)], ["qh%d%d" % (r, k)])
            send(p, "c%d%d" % (k, r), T["ql%d" % r][:, lo:hi].bitcast(dt.uint8), T["qh%d" % r][:, lo:hi].bitcast(dt.uint8), ["qh%d%d" % (r, k)])
            send(p, "s%d%d" % (k, r), T["sl%d" % r][:, lo:hi], T["sh%d" % r][:, lo:hi], ["qh%d%d" % (r, k)])

        def evac(k, i, q):
            lo, hi = CH[k]
            src, dst, pk_ = T[("ph", "pd")[k]][:, 512 * i:512 * i + hi - lo], T.hh[:, 4 * lo + i:4 * hi:4], "P" + "hd"[k] + str(i)
            if q == "s": act(dst, src, [pk_], ["hh%d%d" % (k, i)], 0.03125)
            else: ts1(dst, src, 0.03125, A.mult, [pk_], ["hh%d%d" % (k, i)])

        for k in range(2):
            for t in range(4): gather_a(k, t)
        for t in range(4): add_b(0, t)
        layer(0, 192, "ph", "qz", "sz", 0, [0], "qz0")
        for t in range(4): add_b(1, t)
        layer(192, 336, "pd", "qz", "sz", 0, [1], "qz1")
        for i in range(4): evac(0, i, "s")
        pack(0)
        for i in range(4): evac(1, i, "vs"[i % 2])
        for t in range(4): gather_a(2, t)
        pack(1)

        def own_part():
            for t in range(4): add_b(2, t)
            layer(OWN[0], OWN[1], "ph", "qo", "so", OWN[0], [1, 2], "qo")
            for i in range(4): act(T.jp[:, C * i + F:C * i + C], T.ph[:, 512 * i + F - OWN[0]:512 * i + C - OWN[0]], ["Ph%d" % i], ["jp%dh" % i], 0.03125)
        if OPT["z3"] == 1: own_part()
        tt(si("is"), col("tcb", 0), col("te", 0), A.add, ["tcb", "te"], ["is"])
        tt(sm("df"), sm("nd"), col("tac", 8), A.subtract, ["nd", "tac"], ["df"])
        ts2(si("odd"), si("is"), 19, A.arith_shift_right, 1, A.bitwise_and, ["is"], ["odd"])
        tt(sm("dfo"), sm("df"), si("odd"), A.mult, ["df", "odd"], ["dfo"])
        tt(sm("dT"), sm("dT"), sm("dfo"), A.add, ["dT", "dfo"], ["dT"])
        last = r == ROUNDS - 1
        fw, fk = (sm("wd"), "wd") if last else (T["lsend%d" % (r + 1)][:, K:2 * K], "ls%dw" % (r + 1))
        if not last: cp(T["lsend%d" % (r + 1)][:, 0:K], sm("dT"), ["dT"], ["ls%dt" % (r + 1)])
        swap("tfb", "r480", "f480", [(sm("dT"), ["dT"])], [(fw, [fk])])
        cp(T.dW[:, :], fw, [fk], ["dW"])
        if last:
            dma("y", "st0", T.dn[:, :], T.r480[0:128:16, 16:16 + C], ["r480"], [])
        else:
            send(peer[r + 1], "l%d" % (r + 1), T["lland%d" % (r + 1)][:, :], T["lsend%d" % (r + 1)][:, :], ["ls%dw" % (r + 1), "ls%dt" % (r + 1)])
        if OPT["scat"] == 3: invert()
        if OPT["z3"] == 0: own_part()
        pick16(T.einv[:, :], T.dW[:, :], ["einv", "dW"])
        fold16(T.lW[:, :], "lW")
        if r == 0:
            for b in range(4): quant(T.qe[:, 128 * b:128 * b + 128], T.se_[:, 128 * b:128 * b + 128], T["et%d" % b][:, :], ["et%d" % b], ["qe%d" % b])
        if last: quant(T.qv[:, :], T.sv_[:, :], T.vb[:, :], ["vb"], ["qv"])
        for k, (lo, hi) in enumerate(CH):
            n = hi - lo
            for b in range(4):
                mm(T[("ph", "pd")[k]][:, 512 * b:512 * b + n], T.qe[:, 128 * b:128 * b + 128], T.se_[:, 128 * b:128 * b + 128], T["ql%d" % r][:, lo:hi], T["sl%d" % r][:, lo:hi],
                   ["qe%d" % b, "ql%d.%d" % (r, k), "sl%d.%d" % (r, k)], ["P" + "hd"[k] + str(b)])
            for b in range(4):
                src, dst, pk_ = T[("ph", "pd")[k]][:, 512 * b:512 * b + n], T.jp[:, C * b + lo:C * b + hi], "P" + "hd"[k] + str(b)
                if k == 0 or b % 2: act(dst, src, [pk_], ["jp%d%d" % (b, k)])
                else: cp(dst, src, [pk_], ["jp%d%d" % (b, k)])
        for t in range(4):
            tt(T[XN][:, t:4 * C:4], T.jp[:, C * t:C * t + C].indirect(T.lW[:, :]), T[X][:, t:4 * C:4], A.add,
               ["jp%d0" % t, "jp%d1" % t, "jp%dh" % t, "lW", X], [XN])

    quant(T.qx[:, :], T.sx[:, :], T.x3[:, :], ["x3"], ["qx"])
    dma("y", "st1", T.oc[:, :], T.qx[:, :].bitcast(dt.uint8), ["qx"], [])
    mm(T.pd[:, 0:C], T.qv[:, :], T.sv_[:, :], T.qx[:, :], T.sx[:, :], ["qv", "qx"], ["Pd0"])
    for k in range(4): dma("y", "st%d" % (2 + k), T.osc[4 * k:4 * k + 4, :], T.sx[32 * k:32 * k + 4, :], ["qx"], [])
    act(T.ysb[:, :], T.pd[:, 0:C], ["Pd0"], ["ysb"])
    dma("s", "st6", T.y[:, :], T.ysb[:, :], ["ysb"], [])
    for s in sorted(count): wait("g", (s, count[s]))
